import numpy as np
import ml_dtypes


def mxq(x, axis, fmt="e4m3"):
    dtype, down = {"e4m3": (ml_dtypes.float8_e4m3fn, 7), "e5m2": (ml_dtypes.float8_e5m2, 14)}[fmt]
    v = np.moveaxis(np.asarray(x, np.float32).astype(ml_dtypes.bfloat16).astype(np.float64), axis, -1)
    blocks = v.reshape(v.shape[:-1] + (-1, 32))
    amax = np.abs(blocks).max(-1, keepdims=True)
    byte = np.maximum(np.where(amax > 0, np.frexp(amax)[1] - 1 + 127, 0) - down, 1)
    scale = np.exp2(byte - 127.0)
    codes = (blocks / scale).astype(np.float32).astype(dtype).astype(np.float64)
    return np.moveaxis((codes * scale).reshape(v.shape), -1, axis)


WIDE = False


def mx_kscale(k):
    if not WIDE:
        return np.ones(k)
    levels = np.array([10, -10, 5, -5, 0])
    if k % 512:
        return np.exp2(np.random.permutation(np.resize(levels, k // 32))).repeat(32)
    a = np.empty((k // 512, 16))
    for p in range(k // 512):
        a[p, :8] = np.random.permutation(np.resize(levels, 8))
        for g in range(8):
            far = levels[np.abs(levels - a[p, g]) >= 10]
            a[p, g + 8] = far[np.random.randint(len(far))]
    return np.exp2(a.ravel()).repeat(32)


BF16 = ml_dtypes.bfloat16


def bf(x):
    return np.asarray(x, np.float32).astype(BF16)


def f64(x):
    return np.asarray(x).astype(np.float64)

def planes(Y):
    n, m = Y.shape
    b = f64(bf(Y)).reshape(n // 32, 32, m)
    amax = np.abs(b).max(1)
    byte = np.clip(np.where(amax > 0, np.frexp(amax)[1] - 1 + 127 - 7, 1), 1, 254)
    codes = (b * np.exp2(127.0 - byte)[:, None, :]).reshape(n, m).astype(np.float32).astype(ml_dtypes.float8_e4m3fn).view(np.uint8)
    words = codes.reshape(n // 512, 128, 4, m).transpose(0, 1, 3, 2)
    return np.ascontiguousarray(words), np.ascontiguousarray(byte.astype(np.uint8).reshape(n // 512, 16, m))


T, D, F, V = 1024, 1024, 2048, 512


def setup_inputs():
    rnd = np.random.standard_normal
    s = mx_kscale(D)
    v = mx_kscale(V)
    t = mx_kscale(T)
    u = np.exp(0.8 * rnd(D))
    x = rnd((T, D)) * s
    w_enc = rnd((D, F)) / np.sqrt(D) / s[:, None]
    b_enc = 0.3 * rnd(F)
    token_weight = np.exp(0.3 * rnd(T)) * T ** -0.25 * t
    logit_cotangent = rnd((T, V)) * T ** -0.25 * v / t[:, None]
    w_unembed = rnd((D, V)) * u[:, None] / np.sqrt(V) / v
    w_dec = 0.5 * rnd((F, D)) * u
    step = np.exp(0.2 * rnd(F))
    return {"x": bf(x), "w_enc": bf(w_enc), "b_enc": bf(b_enc),
            "token_weight": bf(token_weight), "logit_cotangent": bf(logit_cotangent),
            "w_unembed": bf(w_unembed), "w_dec": bf(w_dec), "step": bf(step)}

def reference(x, w_enc, b_enc, token_weight, logit_cotangent, w_unembed, w_dec, step):
    pre = mxq(f64(x), 1, "e4m3") @ mxq(f64(w_enc), 0, "e4m3")
    a = np.maximum(pre + f64(b_enc), 0.0) * f64(token_weight)[:, None]
    g = mxq(f64(logit_cotangent), 1, "e4m3") @ mxq(f64(w_unembed), 1, "e4m3").T
    grad = mxq(a, 0, "e4m3").T @ mxq(g, 0, "e4m3")
    y = f64(w_dec) - f64(step)[:, None] * grad
    words, scales = planes(y.T)
    return y, words, scales

@@ -1,0 +1,526 @@
+from contextlib import ExitStack
+
+import concourse.mybir as mybir
+from concourse.masks import make_identity
+
+T, D, F, V = 1024, 1024, 2048, 512
+FLOPS = 2 * T * D * F + 2 * T * V * D + 2 * F * T * D
+
+F32 = mybir.dt.float32
+BF16 = mybir.dt.bfloat16
+U32 = mybir.dt.uint32
+I32 = mybir.dt.int32
+U8 = mybir.dt.uint8
+FP8X4 = mybir.dt.float8_e4m3fn_x4
+ALU = mybir.AluOpType
+ACT = mybir.ActivationFunctionType
+
+P = 128
+KP = 512
+TILES = F // P
+LAG = 5
+WORD_BATCHES = ((0, 4), (4, 8), (8, 12), (12, 15), (15, 16))
+SCALE_BATCHES = ((0, 12), (12, 16))
+W_ON_SCALAR = (7,9,11,13,15)
+MX_BANKS = (0, 1, 2, 3, 4)
+TR_BANKS = (5, 6, 7)
+
+
+def tile_sae_decoder_logit_step_h3_kernel(
+    tc, x, w_enc, b_enc, token_weight, logit_cotangent, w_unembed, w_dec, step, out_0, out_1, out_2
+):
+    nc = tc.nc
+    with ExitStack() as ctx:
+        keep = ctx.enter_context(tc.tile_pool(name="keep", bufs=1))
+        work = ctx.enter_context(tc.tile_pool(name="work", bufs=3))
+        psum = ctx.enter_context(tc.psum_pool(name="psum", bufs=1))
+        ctx.enter_context(tc.manual_schedule())
+
+        turn = {"mx": 0, "tr": 0}
+
+        def bank(kind):
+            banks = MX_BANKS if kind == "mx" else TR_BANKS
+            number = banks[turn[kind] % len(banks)]
+            turn[kind] = turn[kind] + 1
+            return psum.tile([P, KP], F32, name="bank%d" % number)
+
+        def planes(name, width, pool=keep, bufs=None):
+            codes = pool.tile([P, width], U32, name=name + "_codes", align_bytes=64, bufs=bufs)
+            scales = pool.tile([P, width], U8, name=name + "_scales", align_bytes=64, bufs=bufs)
+            return codes, scales
+
+        def quantize(dst, first, src):
+            codes, scales = dst
+            cols = slice(first, first + src.shape[1] // 4)
+            nc.vector.quantize_mx(out=codes[:, cols].bitcast(FP8X4), scales=scales[:, cols], in_=src)
+
+        def mx(out, stationary, s_first, moving, m_first, width, start, stop):
+            s_cols = slice(s_first, s_first + P)
+            m_cols = slice(m_first, m_first + width)
+            nc.tensor.matmul_mx(
+                out=out,
+                lhsT=stationary[0][:, s_cols].bitcast(FP8X4),
+                lhsT_scale=stationary[1][:, s_cols],
+                rhs=moving[0][:, m_cols].bitcast(FP8X4),
+                rhs_scale=moving[1][:, m_cols],
+                start=start,
+                stop=stop,
+            )
+
+        tw_raw = keep.tile([P, 2, 4], BF16, name="tw_raw")
+        nc.scalar.dma_start(out=tw_raw[:], in_=token_weight.rearrange("(g p j) -> p g j", g=2, j=4))
+        rows_raw = keep.tile([32, P], BF16, name="rows_raw")
+        nc.scalar.dma_start(out=rows_raw[0:TILES, :], in_=b_enc.rearrange("(i p) -> i p", p=P))
+        nc.scalar.dma_start(out=rows_raw[TILES : 2 * TILES, :], in_=step.rearrange("(i p) -> i p", p=P))
+
+        x_raw, w_raw, lc_raw, wu_raw, wd_raw = {}, {}, {}, {}, {}
+
+        def load_x(g, u):
+            x_raw[g, u] = keep.tile([P, 2, D], BF16, name="x_raw%d%d" % (g, u))
+            rows = x[KP * g : KP * (g + 1), :].rearrange("(p u e) d -> p u e d", u=2, e=2)
+            nc.sync.dma_start(out=x_raw[g, u][:], in_=rows[:, u, :, :])
+
+        def load_w(k):
+            for c in range(2):
+                w_raw[k, c] = keep.tile([P, 4, KP], BF16, name="w_raw%d%d" % (k, c))
+                rows = w_enc[KP * c : KP * (c + 1), KP * k : KP * (k + 1)]
+                nc.sync.dma_start(out=w_raw[k, c][:], in_=rows.rearrange("(p j) f -> p j f", j=4))
+
+        def load_lc(g):
+            lc_raw[g] = keep.tile([P, 4, V], BF16, name="lc_raw%d" % g)
+            rows = logit_cotangent[KP * g : KP * (g + 1), :]
+            nc.sync.dma_start(out=lc_raw[g][:], in_=rows.rearrange("(p j) v -> p j v", j=4))
+
+        def load_wu(h):
+            wu_raw[h] = keep.tile([P, 2, 2, V], BF16, name="wu_raw%d" % h)
+            rows = w_unembed[KP * h : KP * (h + 1), :]
+            nc.sync.dma_start(out=wu_raw[h][:], in_=rows.rearrange("(a p j) v -> p a j v", a=2, j=2))
+
+        def load_wd(q):
+            wd_raw[q] = work.tile([P, 2, D], BF16, name="wd_raw", bufs=4)
+            rows = w_dec[2 * P * q : 2 * P * (q + 1), :]
+            nc.sync.dma_start(out=wd_raw[q][:], in_=rows.rearrange("(a p) d -> p a d", a=2))
+
+        load_lc(0)
+        load_wu(0)
+        load_x(0, 0)
+        load_x(0, 1)
+        load_w(0)
+        load_x(1, 0)
+        load_x(1, 1)
+        load_lc(1)
+        load_wu(1)
+        load_w(1)
+        load_wd(0)
+        load_w(2)
+        load_wd(1)
+        load_w(3)
+        load_wd(2)
+        load_wd(3)
+
+        ident = keep.tile([P, P], F32, name="ident")
+        make_identity(nc, ident[:])
+        rows32 = keep.tile([P, P], F32, name="rows32")
+        nc.gpsimd.memset(rows32[:], 0.0)
+        tw32 = keep.tile([P, 8], F32, name="tw32")
+        half_sign = keep.tile([P, 8], F32, name="half_sign")
+        bias = keep.tile([P, TILES], F32, name="bias")
+        minus_step = keep.tile([P, TILES], F32, name="minus_step")
+        tw_abs = keep.tile([P, T], BF16, name="tw_abs")
+
+        def small_prepare():
+            nc.vector.tensor_copy(out=tw32[:], in_=tw_raw[:].rearrange("p g j -> p (g j)"))
+            nc.vector.tensor_copy(out=rows32[0:32, :], in_=rows_raw[:])
+            nc.vector.tensor_scalar(
+                out=half_sign[:], in0=tw_raw[:].rearrange("p g j -> p (g j)"), scalar1=0.0, scalar2=0.5,
+                op0=ALU.is_ge, op1=ALU.subtract,
+            )
+
+        def small_turn():
+            turned = bank("mx")
+            nc.tensor.transpose(turned[:, 0:P], rows32[:], ident[:])
+            nc.vector.tensor_copy(out=bias[:], in_=turned[:, 0:TILES])
+            nc.vector.tensor_scalar(
+                out=minus_step[:], in0=turned[:, TILES : 2 * TILES], scalar1=-1.0, scalar2=None, op0=ALU.mult
+            )
+            for g in range(2):
+                spread = bank("mx")
+                for j in range(4):
+                    column = tw32[:, 4 * g + j : 4 * g + j + 1].to_broadcast([P, P])
+                    nc.tensor.transpose(spread[:, P * j : P * (j + 1)], column, ident[:])
+                nc.scalar.activation(
+                    out=tw_abs[:, KP * g : KP * (g + 1)].rearrange("m (u p e) -> m u p e", u=2, e=2),
+                    in_=spread[:].rearrange("m (u e p) -> m u p e", u=2, e=2),
+                    func=ACT.Abs,
+                )
+
+        def turn_rows(sources, name, engine, kind="tr"):
+            turned = bank(kind)
+            for n in range(4):
+                nc.tensor.transpose(turned[:, P * n : P * (n + 1)], sources[n], ident[:])
+            return turned
+
+        x_q = {(g, c): planes("x%d%d" % (g, c), KP) for g in range(2) for c in range(2)}
+        lc_q = {g: planes("lc%d" % g, KP) for g in range(2)}
+        wu_q = {h: planes("wu%d" % h, KP) for h in range(2)}
+        g_q = {(g, h): planes("g%d%d" % (g, h), KP) for g in range(2) for h in range(2)}
+        w_q, a_q, staged = {}, {}, {}
+
+        def copy_on(engine, out, in_):
+            if engine == "scalar":
+                nc.scalar.copy(out=out, in_=in_)
+            else:
+                nc.vector.tensor_copy(out=out, in_=in_)
+
+        def x_turn(g, u, c, engine, kind="tr"):
+            if ("xs", g, u, c) in staged:
+                words = staged["xs", g, u, c]
+                sources = [words[:, P * n : P * (n + 1)] for n in range(4)]
+            else:
+                words = x_raw[g, u][:].bitcast(F32)
+                sources = [words[:, e, 256 * c + w : 256 * (c + 1) : 2] for e in range(2) for w in range(2)]
+            turned = turn_rows(sources, "x", "scalar", kind)
+            grouped = work.tile([P, 1024], BF16, name="grouped", bufs=6, align_bytes=64)
+            staged["x", g, u, c] = grouped
+            copy_on(
+                engine,
+                grouped[:].bitcast(F32).rearrange("k (p e w) -> k p e w", e=2, w=2),
+                turned[:].rearrange("k (e w p) -> k p e w", e=2, w=2),
+            )
+
+        def x_sort(g, u, c, engine):
+            ordered = work.tile([P, KP], F32, name="ordered", bufs=3)
+            staged["xs", g, u, c] = ordered
+            words = x_raw[g, u][:].bitcast(F32)[:, :, 256 * c : 256 * (c + 1)]
+            copy_on(engine, ordered[:].rearrange("k (e w p) -> k e w p", e=2, w=2), words.rearrange("k e (p w) -> k e w p", w=2))
+
+        def wu_sort(h, a, engine):
+            ordered = work.tile([P, KP], F32, name="ordered", bufs=3)
+            staged["wus", h, a] = ordered
+            words = wu_raw[h][:].bitcast(F32)[:, a, :, :]
+            copy_on(engine, ordered[:].rearrange("k (e w p) -> k e w p", e=2, w=2), words.rearrange("k e (p w) -> k e w p", w=2))
+
+        def x_quant(g, u, c):
+            quantize(x_q[g, c], 256 * u, staged["x", g, u, c][:])
+
+        def lc_sign(g):
+            signed = work.tile([P, 4, V], BF16, name="signed", bufs=2)
+            staged["signed", g] = signed
+            for j in range(4):
+                nc.vector.tensor_scalar(
+                    out=signed[:, j, :].rearrange("p (w c e) -> p w c e", w=2, e=2),
+                    in0=lc_raw[g][:, j, :].rearrange("p (c w e) -> p w c e", w=2, e=2),
+                    scalar1=half_sign[:, 4 * g + j : 4 * g + j + 1], scalar2=2.0, op0=ALU.mult, op1=ALU.mult,
+                )
+
+        def lc_turn(g, a, engine):
+            words = staged["signed", g][:].rearrange("p j v -> p (j v)").bitcast(F32)
+            turned = turn_rows([words[:, P * n : P * (n + 1)] for n in range(4 * a, 4 * a + 4)], "lc", "scalar")
+            grouped = work.tile([P, 1024], BF16, name="grouped", bufs=6, align_bytes=64)
+            staged["lc", g, a] = grouped
+            copy_on(
+                engine,
+                grouped[:].bitcast(F32).rearrange("k (j p w) -> k j p w", j=2, w=2),
+                turned[:].rearrange("k (j w p) -> k j p w", j=2, w=2),
+            )
+
+        def lc_quant(g, a):
+            quantize(lc_q[g], 256 * a, staged["lc", g, a][:])
+
+        def wu_turn(h, a, engine):
+            if ("wus", h, a) in staged:
+                words = staged["wus", h, a]
+                sources = [words[:, P * n : P * (n + 1)] for n in range(4)]
+            else:
+                words = wu_raw[h][:].bitcast(F32)
+                sources = [words[:, a, j, w:256:2] for j in range(2) for w in range(2)]
+            turned = turn_rows(sources, "wu", "scalar")
+            grouped = work.tile([P, 1024], BF16, name="grouped", bufs=6, align_bytes=64)
+            staged["wu", h, a] = grouped
+            copy_on(
+                engine,
+                grouped[:].bitcast(F32).rearrange("k (p j w) -> k p j w", j=2, w=2),
+                turned[:].rearrange("k (j w p) -> k p j w", j=2, w=2),
+            )
+
+        def wu_quant(h, a):
+            quantize(wu_q[h], 256 * a, staged["wu", h, a][:])
+
+        def g_mult(g, h, a):
+            grouped = work.tile([P, 1024], BF16, name="grouped", bufs=6, align_bytes=64)
+            staged["g", g, h, a] = grouped
+            for b in range(2):
+                acc = bank("mx")
+                for t in range(4):
+                    mx(acc[:, P * t : P * (t + 1)], lc_q[g], P * t, wu_q[h], 256 * a + P * b, P, True, True)
+                nc.scalar.copy(
+                    out=grouped[:, KP * b : KP * (b + 1)].rearrange("p (d t) -> p d t", t=4),
+                    in_=acc[:].rearrange("p (t d) -> p d t", t=4),
+                )
+
+        def g_quant(g, h, a):
+            quantize(g_q[g, h], 256 * a, staged["g", g, h, a][:])
+
+        def w_group(n, engine):
+            q, c = divmod(n, 2)
+            grouped = work.tile([P, 1024], BF16, name="w_grouped", bufs=3, align_bytes=64)
+            staged["w", n] = grouped
+            cols = slice(256 * (q % 2), 256 * (q % 2 + 1))
+            copy_on(
+                engine,
+                grouped[:].rearrange("p (a i t) -> p a t i", i=4, t=4),
+                w_raw[q // 2, c][:, :, cols].rearrange("p t (a i) -> p a t i", i=4),
+            )
+
+        def w_quant(n):
+            w_q[n] = planes("w", 256, work, 8)
+            quantize(w_q[n], 0, staged["w", n][:])
+
+        def a_half(i, g):
+            acc = bank("mx")
+            staged["pre", i, g] = acc
+            for c in range(2):
+                mx(acc[:], w_q[2 * (i // 2) + c], P * (i % 2), x_q[g, c], 0, KP, c == 0, c == 1)
+
+        def a_scale(i, g):
+            if g == 0:
+                staged["at", i] = work.tile([P, T], BF16, name="a_t", bufs=3)
+            nc.vector.scalar_tensor_tensor(
+                out=staged["at", i][:, KP * g : KP * (g + 1)], in0=staged["pre", i, g][:], scalar=bias[:, i : i + 1],
+                in1=tw_abs[:, KP * g : KP * (g + 1)], op0=ALU.add, op1=ALU.mult,
+            )
+
+        def a_turn(i):
+            words = staged["at", i][:].bitcast(F32)
+            turned = turn_rows(
+                [words[:, 256 * g + P * u : 256 * g + P * (u + 1)] for u in range(2) for g in range(2)], "a", "scalar"
+            )
+            staged["aturned", i] = turned
+
+        def a_relu(i):
+            grouped = work.tile([P, 1024], BF16, name="a_grouped", bufs=3, align_bytes=64)
+            staged["a", i] = grouped
+            nc.scalar.activation(
+                out=grouped[:].rearrange("p (m u e) -> p m u e", u=2, e=2),
+                in_=staged["aturned", i][:].bitcast(BF16).rearrange("p (u m e) -> p m u e", u=2, e=2),
+                func=ACT.Relu,
+            )
+
+        def a_quant(i):
+            a_q[i] = planes("a", 256, work, LAG + 2)
+            quantize(a_q[i], 0, staged["a", i][:])
+
+        def y_mult(i):
+            for h in range(2):
+                acc = bank("mx")
+                staged["grad", i, h] = acc
+                for g in range(2):
+                    mx(acc[:], a_q[i], P * g, g_q[g, h], 0, KP, g == 0, g == 1)
+
+        def y_step(i, h):
+            if h == 0:
+                staged["y", i] = work.tile([P, D], F32, name="y", bufs=5)
+            cols = slice(KP * h, KP * (h + 1))
+            nc.vector.scalar_tensor_tensor(
+                out=staged["y", i][:, cols], in0=staged["grad", i, h][:], scalar=minus_step[:, i : i + 1],
+                in1=wd_raw[i // 2][:, i % 2, cols], op0=ALU.mult, op1=ALU.add,
+            )
+
+        def y_store(i):
+            nc.sync.dma_start(out=out_0[P * i : P * (i + 1), :], in_=staged["y", i][:])
+            if i % 2 == 1 and i // 2 + 4 < TILES // 2:
+                load_wd(i // 2 + 4)
+
+        def y_round(i):
+            rounded = work.tile([P, D], BF16, name="y_rounded", bufs=3)
+            staged["yr", i] = rounded
+            nc.scalar.copy(
+                out=rounded[:].rearrange("m (u c e) -> m u c e", u=2, e=2),
+                in_=staged["y", i][:].rearrange("m (c u e) -> m u c e", u=2, e=2),
+            )
+
+        def y_turn(i):
+            words = staged["yr", i][:].bitcast(F32)
+            staged["yturned", i] = turn_rows([words[:, P * n : P * (n + 1)] for n in range(4)], "y", "scalar")
+
+        def y_group(i, engine):
+            grouped = work.tile([P, 1024], BF16, name="y_grouped", bufs=3, align_bytes=64)
+            staged["yg", i] = grouped
+            copy_on(
+                engine,
+                grouped[:].bitcast(F32).rearrange("p (m u) -> p m u", u=2),
+                staged["yturned", i][:].rearrange("p (u m) -> p m u", u=2),
+            )
+
+        def y_finish_round(i, g, engine):
+            rounded = work.tile([P, KP], BF16, name="y_rounded", bufs=3)
+            staged["yr", i, g] = rounded
+            copy_on(
+                engine,
+                rounded[:].rearrange("m (u c e) -> m u c e", u=2, e=2),
+                staged["y", i][:, KP * g : KP * (g + 1)].rearrange("m (c u e) -> m u c e", u=2, e=2),
+            )
+
+        def y_finish_turn(i, g, engine):
+            words = staged["yr", i, g][:].bitcast(F32)
+            turned = bank("tr")
+            for u in range(2):
+                nc.tensor.transpose(turned[:, P * u : P * (u + 1)], words[:, P * u : P * (u + 1)], ident[:])
+            if g == 0:
+                staged["yg", i] = work.tile([P, 1024], BF16, name="y_grouped", bufs=3, align_bytes=64)
+            copy_on(
+                engine,
+                staged["yg", i][:, KP * g : KP * (g + 1)].bitcast(F32).rearrange("p (m u) -> p m u", u=2),
+                turned[:, 0 : 2 * P].rearrange("p (u m) -> p m u", u=2),
+            )
+
+        words_out = out_1.rearrange("g p m t -> p g (m t)").bitcast(I32)
+        scales_out = out_2.rearrange("g q m -> q g m").bitcast(I32)
+        word_batch = {i: (first, last) for first, last in WORD_BATCHES for i in range(first, last)}
+        scale_batch = {i: (first, last) for first, last in SCALE_BATCHES for i in range(first, last)}
+
+        def y_quant(i, groups=(0, 1)):
+            w_first, w_last = word_batch[i]
+            s_first, s_last = scale_batch[i]
+            if i == w_first and 0 in groups:
+                staged["ycodes"] = work.tile([P, 2, P * (w_last - w_first)], U32, name="y_codes", bufs=2, align_bytes=64)
+            if i == s_first and 0 in groups:
+                staged["yscales"] = keep.tile([P, 2, P * (s_last - s_first)], U8, name="y_scales%d" % i, align_bytes=64)
+            for g in groups:
+                nc.vector.quantize_mx(
+                    out=staged["ycodes"][:, g, P * (i - w_first) : P * (i - w_first + 1)].bitcast(FP8X4),
+                    scales=staged["yscales"][:, g, P * (i - s_first) : P * (i - s_first + 1)],
+                    in_=staged["yg", i][:, KP * g : KP * (g + 1)],
+                )
+            if i == w_last - 1 and 1 in groups:
+                nc.sync.dma_start(out=words_out[:, :, P * w_first : P * w_last], in_=staged["ycodes"][:].bitcast(I32))
+            if i == s_last - 1 and 1 in groups:
+                for quad in range(4):
+                    nc.sync.dma_start(
+                        out=scales_out[4 * quad : 4 * quad + 4, :, P * s_first // 4 : P * s_last // 4],
+                        in_=staged["yscales"][32 * quad : 32 * quad + 4, :, :].bitcast(I32),
+                    )
+
+        small_prepare()
+        small_turn()
+        lc_sign(0)
+        wu_sort(0, 0, "scalar")
+        wu_sort(0, 1, "scalar")
+        lc_turn(0, 0, "vector")
+        lc_turn(0, 1, "vector")
+        x_sort(0, 0, 0, "scalar")
+        wu_turn(0, 0, "scalar")
+        lc_quant(0, 0)
+        lc_quant(0, 1)
+        wu_turn(0, 1, "vector")
+        wu_quant(0, 0)
+        x_turn(0, 0, 0, "scalar")
+        x_turn(0, 0, 1, "vector")
+        wu_quant(0, 1)
+        g_mult(0, 0, 0)
+        x_quant(0, 0, 0)
+        x_quant(0, 0, 1)
+        w_group(0, "vector")
+        x_turn(0, 1, 0, "vector")
+        x_turn(0, 1, 1, "scalar")
+        w_quant(0)
+        w_group(1, "vector")
+        g_mult(0, 0, 1)
+        x_quant(0, 1, 0)
+        x_quant(0, 1, 1)
+        w_quant(1)
+        x_turn(1, 0, 0, "scalar")
+        x_turn(1, 0, 1, "scalar")
+        g_quant(0, 0, 0)
+        a_half(0, 0)
+        a_half(1, 0)
+        g_quant(0, 0, 1)
+        x_quant(1, 0, 0)
+        lc_sign(1)
+        x_quant(1, 0, 1)
+        x_turn(1, 1, 0, "scalar")
+        x_turn(1, 1, 1, "scalar")
+        a_scale(0, 0)
+        x_quant(1, 1, 0)
+        a_scale(1, 0)
+        x_quant(1, 1, 1)
+        lc_turn(1, 0, "scalar")
+        lc_turn(1, 1, "scalar")
+        w_group(2, "vector")
+
+        def live(i):
+            return 0 <= i < TILES
+
+        g_rest = [(1, 0, 0), (1, 0, 1), (0, 1, 0), (0, 1, 1), (1, 1, 0), (1, 1, 1)]
+        g_plan = {0: g_rest[0:1], 1: g_rest[1:2], 2: g_rest[2:4], 3: g_rest[4:6]}
+
+        for n in range(TILES + LAG - 1):
+            j = n - LAG
+            unit = n + 3
+            if live(n):
+                if n > 1:
+                    a_half(n, 0)
+                a_half(n, 1)
+            if live(j):
+                y_mult(j)
+            if live(n - 2):
+                a_relu(n - 2)
+            if live(j - 3):
+                y_group(j - 3, "scalar" if n < TILES + 9 else "vector")
+            if live(j - 1):
+                y_round(j - 1)
+            if n == 0:
+                lc_quant(1, 0)
+                lc_quant(1, 1)
+            if n == 1:
+                wu_quant(1, 0)
+                wu_quant(1, 1)
+            if 2 < unit < TILES:
+                w_group(unit, "scalar" if unit in W_ON_SCALAR else "vector")
+            if live(n):
+                if n > 1:
+                    a_scale(n, 0)
+                a_scale(n, 1)
+            for quarter in g_plan.get(n - 1, []):
+                g_quant(*quarter)
+            for quarter in g_plan.get(n, []):
+                g_mult(*quarter)
+            if unit - 1 < TILES:
+                w_quant(unit - 1)
+            if live(n - 2):
+                a_quant(n - 2)
+            if live(j):
+                y_step(j, 0)
+            if live(j - 3):
+                y_quant(j - 3)
+            if live(j):
+                y_step(j, 1)
+                y_store(j)
+            if live(n - 1):
+                a_turn(n - 1)
+            if live(j - 2):
+                y_turn(j - 2)
+            if n == 0:
+                wu_turn(1, 0, "scalar")
+                wu_turn(1, 1, "scalar")
+
+        last = TILES - 1
+        y_mult(last)
+        y_round(last - 1)
+        y_group(last - 3, "vector")
+        y_step(last, 0)
+        y_turn(last - 2)
+        y_quant(last - 3)
+        y_step(last, 1)
+        y_store(last)
+        y_finish_round(last, 0, "scalar")
+        y_turn(last - 1)
+        y_group(last - 2, "vector")
+        y_finish_round(last, 1, "scalar")
+        y_quant(last - 2)
+        y_group(last - 1, "vector")
+        y_finish_turn(last, 0, "scalar")
+        y_finish_turn(last, 1, "scalar")
+        y_quant(last - 1)
+        y_quant(last, (0,))
+        y_quant(last, (1,))

@@ -18,12 +18,13 @@ ACT = mybir.ActivationFunctionType
 P = 128
 KP = 512
 TILES = F // P
-LAG = 5
-WORD_BATCHES = ((0, 4), (4, 8), (8, 12), (12, 15), (15, 16))
-SCALE_BATCHES = ((0, 12), (12, 16))
-W_ON_SCALAR = (7,9,11,13,15)
-MX_BANKS = (0, 1, 2, 3, 4)
-TR_BANKS = (5, 6, 7)
+PAIRS = TILES // 2
+LAG = 3
+WORD_BATCHES = ((0, 4), (4, 8), (8, 12), (12, 14), (14, 16))
+SCALE_BATCHES = ((0, 10), (10, 16))
+MX_BANKS = (0, 1, 2, 3)
+TR_BANKS = (4, 5, 6, 7)
+POOL_HALVES = 4
 
 
 def tile_sae_decoder_logit_step_h3_kernel(
@@ -34,12 +35,13 @@ def tile_sae_decoder_logit_step_h3_kernel(
         keep = ctx.enter_context(tc.tile_pool(name="keep", bufs=1))
         work = ctx.enter_context(tc.tile_pool(name="work", bufs=3))
         psum = ctx.enter_context(tc.psum_pool(name="psum", bufs=1))
-        ctx.enter_context(tc.manual_schedule())
 
-        turn = {"mx": 0, "tr": 0}
+        turn = {"mx": 0, "tr": 0, "any": 0, "head": 1}
 
         def bank(kind):
-            banks = MX_BANKS if kind == "mx" else TR_BANKS
+            if turn["head"]:
+                kind = "any"
+            banks = {"mx": MX_BANKS, "tr": TR_BANKS, "any": MX_BANKS + TR_BANKS}[kind]
             number = banks[turn[kind] % len(banks)]
             turn[kind] = turn[kind] + 1
             return psum.tile([P, KP], F32, name="bank%d" % number)
@@ -68,7 +70,6 @@ def tile_sae_decoder_logit_step_h3_kernel(
             )
 
         tw_raw = keep.tile([P, 2, 4], BF16, name="tw_raw")
-        nc.scalar.dma_start(out=tw_raw[:], in_=token_weight.rearrange("(g p j) -> p g j", g=2, j=4))
         rows_raw = keep.tile([32, P], BF16, name="rows_raw")
         nc.scalar.dma_start(out=rows_raw[0:TILES, :], in_=b_enc.rearrange("(i p) -> i p", p=P))
         nc.scalar.dma_start(out=rows_raw[TILES : 2 * TILES, :], in_=step.rearrange("(i p) -> i p", p=P))
@@ -97,26 +98,27 @@ def tile_sae_decoder_logit_step_h3_kernel(
             nc.sync.dma_start(out=wu_raw[h][:], in_=rows.rearrange("(a p j) v -> p a j v", a=2, j=2))
 
         def load_wd(q):
-            wd_raw[q] = work.tile([P, 2, D], BF16, name="wd_raw", bufs=4)
+            wd_raw[q] = work.tile([P, 2, D], BF16, name="wd_raw", bufs=3)
             rows = w_dec[2 * P * q : 2 * P * (q + 1), :]
             nc.sync.dma_start(out=wd_raw[q][:], in_=rows.rearrange("(a p) d -> p a d", a=2))
 
-        load_lc(0)
-        load_wu(0)
-        load_x(0, 0)
-        load_x(0, 1)
-        load_w(0)
-        load_x(1, 0)
-        load_x(1, 1)
-        load_lc(1)
-        load_wu(1)
-        load_w(1)
-        load_wd(0)
-        load_w(2)
-        load_wd(1)
-        load_w(3)
-        load_wd(2)
-        load_wd(3)
+        with tc.manual_schedule(engines={mybir.EngineType.SP}):
+            nc.sync.dma_start(out=tw_raw[:], in_=token_weight.rearrange("(g p j) -> p g j", g=2, j=4))
+            load_lc(0)
+            load_wu(0)
+            load_x(0, 0)
+            load_x(0, 1)
+            load_w(0)
+            load_x(1, 0)
+            load_x(1, 1)
+            load_lc(1)
+            load_wu(1)
+            load_w(1)
+            load_wd(0)
+            load_w(2)
+            load_wd(1)
+            load_w(3)
+            load_wd(2)
 
         ident = keep.tile([P, P], F32, name="ident")
         make_identity(nc, ident[:])
@@ -128,31 +130,44 @@ def tile_sae_decoder_logit_step_h3_kernel(
         minus_step = keep.tile([P, TILES], F32, name="minus_step")
         tw_abs = keep.tile([P, T], BF16, name="tw_abs")
 
-        def small_prepare():
-            nc.vector.tensor_copy(out=tw32[:], in_=tw_raw[:].rearrange("p g j -> p (g j)"))
-            nc.vector.tensor_copy(out=rows32[0:32, :], in_=rows_raw[:])
+        def weight_prepare():
             nc.vector.tensor_scalar(
                 out=half_sign[:], in0=tw_raw[:].rearrange("p g j -> p (g j)"), scalar1=0.0, scalar2=0.5,
                 op0=ALU.is_ge, op1=ALU.subtract,
             )
+            nc.vector.tensor_copy(out=tw32[:], in_=tw_raw[:].rearrange("p g j -> p (g j)"))
 
-        def small_turn():
+            nc.vector.tensor_copy(out=rows32[0:32, :], in_=rows_raw[:])
+
+        def weight_spread(g):
+            spread = bank("mx")
+            for j in range(4):
+                column = tw32[:, 4 * g + j : 4 * g + j + 1].to_broadcast([P, P])
+                nc.tensor.transpose(spread[:, P * j : P * (j + 1)], column, ident[:])
+            nc.scalar.activation(
+                out=tw_abs[:, KP * g : KP * (g + 1)].rearrange("m (u p e) -> m u p e", u=2, e=2),
+                in_=spread[:].rearrange("m (u e p) -> m u p e", u=2, e=2),
+                func=ACT.Abs,
+            )
+
+        def rows_turn():
             turned = bank("mx")
             nc.tensor.transpose(turned[:, 0:P], rows32[:], ident[:])
             nc.vector.tensor_copy(out=bias[:], in_=turned[:, 0:TILES])
             nc.vector.tensor_scalar(
                 out=minus_step[:], in0=turned[:, TILES : 2 * TILES], scalar1=-1.0, scalar2=None, op0=ALU.mult
             )
-            for g in range(2):
-                spread = bank("mx")
-                for j in range(4):
-                    column = tw32[:, 4 * g + j : 4 * g + j + 1].to_broadcast([P, P])
-                    nc.tensor.transpose(spread[:, P * j : P * (j + 1)], column, ident[:])
-                nc.scalar.activation(
-                    out=tw_abs[:, KP * g : KP * (g + 1)].rearrange("m (u p e) -> m u p e", u=2, e=2),
-                    in_=spread[:].rearrange("m (u e p) -> m u p e", u=2, e=2),
-                    func=ACT.Abs,
-                )
+
+        def staging(key, half):
+            if key not in staged:
+                staged[key] = work.tile([P, 2048], BF16, name="grouped", bufs=5, align_bytes=64)
+            return staged[key][:, 1024 * half : 1024 * (half + 1)]
+
+        def quant(key, dst, half=None):
+            if half is None:
+                quantize(dst, 0, staged[key][:])
+            else:
+                quantize(dst, 256 * half, staged[key][:, 1024 * half : 1024 * (half + 1)])
 
         def turn_rows(sources, name, engine, kind="tr"):
             turned = bank(kind)
@@ -172,39 +187,39 @@ def tile_sae_decoder_logit_step_h3_kernel(
             else:
                 nc.vector.tensor_copy(out=out, in_=in_)
 
-        def x_turn(g, u, c, engine, kind="tr"):
+        def x_turn(g, u, c):
             if ("xs", g, u, c) in staged:
                 words = staged["xs", g, u, c]
                 sources = [words[:, P * n : P * (n + 1)] for n in range(4)]
             else:
                 words = x_raw[g, u][:].bitcast(F32)
                 sources = [words[:, e, 256 * c + w : 256 * (c + 1) : 2] for e in range(2) for w in range(2)]
-            turned = turn_rows(sources, "x", "scalar", kind)
-            grouped = work.tile([P, 1024], BF16, name="grouped", bufs=6, align_bytes=64)
-            staged["x", g, u, c] = grouped
+            staged["xt", g, u, c] = turn_rows(sources, "x", "scalar")
+
+        def x_group(g, u, c, engine):
             copy_on(
                 engine,
-                grouped[:].bitcast(F32).rearrange("k (p e w) -> k p e w", e=2, w=2),
-                turned[:].rearrange("k (e w p) -> k p e w", e=2, w=2),
+                staging(("x", g, c), u).bitcast(F32).rearrange("k (p e w) -> k p e w", e=2, w=2),
+                staged["xt", g, u, c][:].rearrange("k (e w p) -> k p e w", e=2, w=2),
             )
 
         def x_sort(g, u, c, engine):
-            ordered = work.tile([P, KP], F32, name="ordered", bufs=3)
+            ordered = work.tile([P, KP], F32, name="ordered", bufs=4)
             staged["xs", g, u, c] = ordered
             words = x_raw[g, u][:].bitcast(F32)[:, :, 256 * c : 256 * (c + 1)]
             copy_on(engine, ordered[:].rearrange("k (e w p) -> k e w p", e=2, w=2), words.rearrange("k e (p w) -> k e w p", w=2))
 
         def wu_sort(h, a, engine):
-            ordered = work.tile([P, KP], F32, name="ordered", bufs=3)
+            ordered = work.tile([P, KP], F32, name="ordered", bufs=4)
             staged["wus", h, a] = ordered
             words = wu_raw[h][:].bitcast(F32)[:, a, :, :]
             copy_on(engine, ordered[:].rearrange("k (e w p) -> k e w p", e=2, w=2), words.rearrange("k e (p w) -> k e w p", w=2))
 
-        def x_quant(g, u, c):
-            quantize(x_q[g, c], 256 * u, staged["x", g, u, c][:])
+        def x_quant(g, c, u=None):
+            quant(("x", g, c), x_q[g, c], u)
 
         def lc_sign(g):
-            signed = work.tile([P, 4, V], BF16, name="signed", bufs=2)
+            signed = work.tile([P, 4, V], BF16, name="signed", bufs=1)
             staged["signed", g] = signed
             for j in range(4):
                 nc.vector.tensor_scalar(
@@ -213,78 +228,80 @@ def tile_sae_decoder_logit_step_h3_kernel(
                     scalar1=half_sign[:, 4 * g + j : 4 * g + j + 1], scalar2=2.0, op0=ALU.mult, op1=ALU.mult,
                 )
 
-        def lc_turn(g, a, engine):
+        def lc_turn(g, a):
             words = staged["signed", g][:].rearrange("p j v -> p (j v)").bitcast(F32)
-            turned = turn_rows([words[:, P * n : P * (n + 1)] for n in range(4 * a, 4 * a + 4)], "lc", "scalar")
-            grouped = work.tile([P, 1024], BF16, name="grouped", bufs=6, align_bytes=64)
-            staged["lc", g, a] = grouped
+            staged["lt", g, a] = turn_rows([words[:, P * n : P * (n + 1)] for n in range(4 * a, 4 * a + 4)], "lc", "scalar")
+
+        def lc_group(g, a, engine):
             copy_on(
                 engine,
-                grouped[:].bitcast(F32).rearrange("k (j p w) -> k j p w", j=2, w=2),
-                turned[:].rearrange("k (j w p) -> k j p w", j=2, w=2),
+                staging(("lc", g), a).bitcast(F32).rearrange("k (j p w) -> k j p w", j=2, w=2),
+                staged["lt", g, a][:].rearrange("k (j w p) -> k j p w", j=2, w=2),
             )
 
-        def lc_quant(g, a):
-            quantize(lc_q[g], 256 * a, staged["lc", g, a][:])
+        def lc_quant(g, a=None):
+            quant(("lc", g), lc_q[g], a)
 
-        def wu_turn(h, a, engine):
+        def wu_turn(h, a):
             if ("wus", h, a) in staged:
                 words = staged["wus", h, a]
                 sources = [words[:, P * n : P * (n + 1)] for n in range(4)]
             else:
                 words = wu_raw[h][:].bitcast(F32)
                 sources = [words[:, a, j, w:256:2] for j in range(2) for w in range(2)]
-            turned = turn_rows(sources, "wu", "scalar")
-            grouped = work.tile([P, 1024], BF16, name="grouped", bufs=6, align_bytes=64)
-            staged["wu", h, a] = grouped
+            staged["ut", h, a] = turn_rows(sources, "wu", "scalar")
+
+        def wu_group(h, a, engine):
             copy_on(
                 engine,
-                grouped[:].bitcast(F32).rearrange("k (p j w) -> k p j w", j=2, w=2),
-                turned[:].rearrange("k (j w p) -> k p j w", j=2, w=2),
+                staging(("wu", h), a).bitcast(F32).rearrange("k (p j w) -> k p j w", j=2, w=2),
+                staged["ut", h, a][:].rearrange("k (j w p) -> k p j w", j=2, w=2),
             )
 
-        def wu_quant(h, a):
-            quantize(wu_q[h], 256 * a, staged["wu", h, a][:])
+        def wu_quant(h, a=None):
+            quant(("wu", h), wu_q[h], a)
 
-        def g_mult(g, h, a):
-            grouped = work.tile([P, 1024], BF16, name="grouped", bufs=6, align_bytes=64)
-            staged["g", g, h, a] = grouped
-            for b in range(2):
-                acc = bank("mx")
-                for t in range(4):
-                    mx(acc[:, P * t : P * (t + 1)], lc_q[g], P * t, wu_q[h], 256 * a + P * b, P, True, True)
-                nc.scalar.copy(
-                    out=grouped[:, KP * b : KP * (b + 1)].rearrange("p (d t) -> p d t", t=4),
-                    in_=acc[:].rearrange("p (t d) -> p d t", t=4),
-                )
+        def g_mult(g, h, n):
+            acc = bank("mx")
+            staged["gt", g, h, n] = acc
+            for t in range(4):
+                mx(acc[:, P * t : P * (t + 1)], lc_q[g], P * t, wu_q[h], P * n, P, True, True)
 
-        def g_quant(g, h, a):
-            quantize(g_q[g, h], 256 * a, staged["g", g, h, a][:])
+        def g_group(g, h, n, engine):
+            grouped = staging(("g", g, h), n // 2)
+            copy_on(
+                engine,
+                grouped[:, KP * (n % 2) : KP * (n % 2 + 1)].rearrange("p (d t) -> p d t", t=4),
+                staged["gt", g, h, n][:].rearrange("p (t d) -> p d t", t=4),
+            )
 
-        def w_group(n, engine):
-            q, c = divmod(n, 2)
-            grouped = work.tile([P, 1024], BF16, name="w_grouped", bufs=3, align_bytes=64)
-            staged["w", n] = grouped
+        def g_quant(g, h, a=None):
+            quant(("g", g, h), g_q[g, h], a)
+
+        def w_group(q, c, engine):
+            if c == 0:
+                staged["w", q] = work.tile([P, 2048], BF16, name="w_grouped", bufs=2, align_bytes=64)
             cols = slice(256 * (q % 2), 256 * (q % 2 + 1))
             copy_on(
                 engine,
-                grouped[:].rearrange("p (a i t) -> p a t i", i=4, t=4),
+                staged["w", q][:, 1024 * c : 1024 * (c + 1)].rearrange("p (a i t) -> p a t i", i=4, t=4),
                 w_raw[q // 2, c][:, :, cols].rearrange("p t (a i) -> p a t i", i=4),
             )
 
-        def w_quant(n):
-            w_q[n] = planes("w", 256, work, 8)
-            quantize(w_q[n], 0, staged["w", n][:])
+        def w_quant(q, c=None):
+            if q not in w_q:
+                w_q[q] = planes("w", KP, work, 3)
+            quant(("w", q), w_q[q], c)
 
         def a_half(i, g):
             acc = bank("mx")
             staged["pre", i, g] = acc
             for c in range(2):
-                mx(acc[:], w_q[2 * (i // 2) + c], P * (i % 2), x_q[g, c], 0, KP, c == 0, c == 1)
+                mx(acc[:], w_q[i // 2], 256 * c + P * (i % 2), x_q[g, c], 0, KP, c == 0, c == 1)
 
         def a_scale(i, g):
             if g == 0:
-                staged["at", i] = work.tile([P, T], BF16, name="a_t", bufs=3)
+                staged["at", i] = work.tile([P, T], BF16, name="a_t", bufs=5)
             nc.vector.scalar_tensor_tensor(
                 out=staged["at", i][:, KP * g : KP * (g + 1)], in0=staged["pre", i, g][:], scalar=bias[:, i : i + 1],
                 in1=tw_abs[:, KP * g : KP * (g + 1)], op0=ALU.add, op1=ALU.mult,
@@ -298,24 +315,25 @@ def tile_sae_decoder_logit_step_h3_kernel(
             staged["aturned", i] = turned
 
         def a_relu(i):
-            grouped = work.tile([P, 1024], BF16, name="a_grouped", bufs=3, align_bytes=64)
-            staged["a", i] = grouped
+            if i % 2 == 0:
+                staged["a", i // 2] = work.tile([P, 2048], BF16, name="grouped", bufs=5, align_bytes=64)
+            grouped = staged["a", i // 2][:, 1024 * (i % 2) : 1024 * (i % 2 + 1)]
             nc.scalar.activation(
                 out=grouped[:].rearrange("p (m u e) -> p m u e", u=2, e=2),
                 in_=staged["aturned", i][:].bitcast(BF16).rearrange("p (u m e) -> p m u e", u=2, e=2),
                 func=ACT.Relu,
             )
 
-        def a_quant(i):
-            a_q[i] = planes("a", 256, work, LAG + 2)
-            quantize(a_q[i], 0, staged["a", i][:])
+        def a_quant(q, half=None):
+            if q not in a_q:
+                a_q[q] = planes("a", KP, work, LAG + 1)
+            quant(("a", q), a_q[q], half)
 
-        def y_mult(i):
-            for h in range(2):
-                acc = bank("mx")
-                staged["grad", i, h] = acc
-                for g in range(2):
-                    mx(acc[:], a_q[i], P * g, g_q[g, h], 0, KP, g == 0, g == 1)
+        def y_half(i, h):
+            acc = bank("mx")
+            staged["grad", i, h] = acc
+            for g in range(2):
+                mx(acc[:], a_q[i // 2], 256 * (i % 2) + P * g, g_q[g, h], 0, KP, g == 0, g == 1)
 
         def y_step(i, h):
             if h == 0:
@@ -328,199 +346,246 @@ def tile_sae_decoder_logit_step_h3_kernel(
 
         def y_store(i):
             nc.sync.dma_start(out=out_0[P * i : P * (i + 1), :], in_=staged["y", i][:])
-            if i % 2 == 1 and i // 2 + 4 < TILES // 2:
-                load_wd(i // 2 + 4)
+            if i % 2 == 1 and i // 2 + 3 < TILES // 2:
+                load_wd(i // 2 + 3)
 
-        def y_round(i):
-            rounded = work.tile([P, D], BF16, name="y_rounded", bufs=3)
-            staged["yr", i] = rounded
-            nc.scalar.copy(
-                out=rounded[:].rearrange("m (u c e) -> m u c e", u=2, e=2),
-                in_=staged["y", i][:].rearrange("m (c u e) -> m u c e", u=2, e=2),
-            )
-
-        def y_turn(i):
-            words = staged["yr", i][:].bitcast(F32)
-            staged["yturned", i] = turn_rows([words[:, P * n : P * (n + 1)] for n in range(4)], "y", "scalar")
-
-        def y_group(i, engine):
-            grouped = work.tile([P, 1024], BF16, name="y_grouped", bufs=3, align_bytes=64)
-            staged["yg", i] = grouped
-            copy_on(
-                engine,
-                grouped[:].bitcast(F32).rearrange("p (m u) -> p m u", u=2),
-                staged["yturned", i][:].rearrange("p (u m) -> p m u", u=2),
-            )
-
-        def y_finish_round(i, g, engine):
-            rounded = work.tile([P, KP], BF16, name="y_rounded", bufs=3)
+        def y_round(i, g, engine):
+            rounded = work.tile([P, KP], BF16, name="y_rounded", bufs=8)
             staged["yr", i, g] = rounded
-            copy_on(
-                engine,
-                rounded[:].rearrange("m (u c e) -> m u c e", u=2, e=2),
-                staged["y", i][:, KP * g : KP * (g + 1)].rearrange("m (c u e) -> m u c e", u=2, e=2),
-            )
+            out = rounded[:].rearrange("m (u c e) -> m u c e", u=2, e=2)
+            in_ = staged["y", i][:, KP * g : KP * (g + 1)].rearrange("m (c u e) -> m u c e", u=2, e=2)
+            if engine == "gpsimd":
+                nc.gpsimd.tensor_scalar(out=out, in0=in_, scalar1=1.0, scalar2=1.0, op0=ALU.mult, op1=ALU.mult)
+            else:
+                copy_on(engine, out, in_)
 
-        def y_finish_turn(i, g, engine):
-            words = staged["yr", i, g][:].bitcast(F32)
+        def y_turn(i, groups=(0, 1)):
             turned = bank("tr")
-            for u in range(2):
-                nc.tensor.transpose(turned[:, P * u : P * (u + 1)], words[:, P * u : P * (u + 1)], ident[:])
-            if g == 0:
-                staged["yg", i] = work.tile([P, 1024], BF16, name="y_grouped", bufs=3, align_bytes=64)
-            copy_on(
-                engine,
-                staged["yg", i][:, KP * g : KP * (g + 1)].bitcast(F32).rearrange("p (m u) -> p m u", u=2),
-                turned[:, 0 : 2 * P].rearrange("p (u m) -> p m u", u=2),
-            )
+            for g in groups:
+                staged["yturned", i, g] = turned
+                words = staged["yr", i, g][:].bitcast(F32)
+                for u in range(2):
+                    first = 256 * g + P * u
+                    nc.tensor.transpose(turned[:, first : first + P], words[:, P * u : P * (u + 1)], ident[:])
+
+        def y_group(i, engine, groups=(0, 1)):
+            if ("yg", i // 2) not in staged:
+                staged["yg", i // 2] = work.tile([P, 2048], BF16, name="y_grouped", bufs=3, align_bytes=64)
+            span = slice(groups[0], groups[-1] + 1)
+            words = staged["yg", i // 2][:].bitcast(F32).rearrange("p (g a m u) -> p g a m u", g=2, a=2, u=2)
+            turned = staged["yturned", i, groups[0]][:].rearrange("p (g u m) -> p g m u", g=2, u=2)
+            copy_on(engine, words[:, span, i % 2, :, :], turned[:, span, :, :])
 
         words_out = out_1.rearrange("g p m t -> p g (m t)").bitcast(I32)
         scales_out = out_2.rearrange("g q m -> q g m").bitcast(I32)
         word_batch = {i: (first, last) for first, last in WORD_BATCHES for i in range(first, last)}
         scale_batch = {i: (first, last) for first, last in SCALE_BATCHES for i in range(first, last)}
 
-        def y_quant(i, groups=(0, 1)):
-            w_first, w_last = word_batch[i]
-            s_first, s_last = scale_batch[i]
-            if i == w_first and 0 in groups:
-                staged["ycodes"] = work.tile([P, 2, P * (w_last - w_first)], U32, name="y_codes", bufs=2, align_bytes=64)
-            if i == s_first and 0 in groups:
-                staged["yscales"] = keep.tile([P, 2, P * (s_last - s_first)], U8, name="y_scales%d" % i, align_bytes=64)
-            for g in groups:
-                nc.vector.quantize_mx(
-                    out=staged["ycodes"][:, g, P * (i - w_first) : P * (i - w_first + 1)].bitcast(FP8X4),
-                    scales=staged["yscales"][:, g, P * (i - s_first) : P * (i - s_first + 1)],
-                    in_=staged["yg", i][:, KP * g : KP * (g + 1)],
+        def y_quant(first, count, g):
+            w_first, w_last = word_batch[first]
+            s_first, s_last = scale_batch[first]
+            if ("ycodes", w_first) not in staged:
+                staged["ycodes", w_first] = work.tile(
+                    [P, 2, P * (w_last - w_first)], U32, name="y_codes", bufs=3, align_bytes=64
                 )
-            if i == w_last - 1 and 1 in groups:
-                nc.sync.dma_start(out=words_out[:, :, P * w_first : P * w_last], in_=staged["ycodes"][:].bitcast(I32))
-            if i == s_last - 1 and 1 in groups:
+            if ("yscales", s_first) not in staged:
+                staged["yscales", s_first] = keep.tile(
+                    [P, 2, P * (s_last - s_first)], U8, name="y_scales%d" % s_first, align_bytes=64
+                )
+            codes, scales = staged["ycodes", w_first], staged["yscales", s_first]
+            end = first + count
+            start = 1024 * g + KP * (first % 2)
+            nc.vector.quantize_mx(
+                out=codes[:, g, P * (first - w_first) : P * (end - w_first)].bitcast(FP8X4),
+                scales=scales[:, g, P * (first - s_first) : P * (end - s_first)],
+                in_=staged["yg", first // 2][:, start : start + KP * count],
+            )
+            if end == w_last and g == 1:
+                nc.sync.dma_start(out=words_out[:, :, P * w_first : P * w_last], in_=codes[:].bitcast(I32))
+            if end == s_last and g == 1:
                 for quad in range(4):
                     nc.sync.dma_start(
                         out=scales_out[4 * quad : 4 * quad + 4, :, P * s_first // 4 : P * s_last // 4],
-                        in_=staged["yscales"][32 * quad : 32 * quad + 4, :, :].bitcast(I32),
+                        in_=scales[32 * quad : 32 * quad + 4, :, :].bitcast(I32),
                     )
 
-        small_prepare()
-        small_turn()
-        lc_sign(0)
-        wu_sort(0, 0, "scalar")
-        wu_sort(0, 1, "scalar")
-        lc_turn(0, 0, "vector")
-        lc_turn(0, 1, "vector")
-        x_sort(0, 0, 0, "scalar")
-        wu_turn(0, 0, "scalar")
-        lc_quant(0, 0)
-        lc_quant(0, 1)
-        wu_turn(0, 1, "vector")
-        wu_quant(0, 0)
-        x_turn(0, 0, 0, "scalar")
-        x_turn(0, 0, 1, "vector")
-        wu_quant(0, 1)
-        g_mult(0, 0, 0)
-        x_quant(0, 0, 0)
-        x_quant(0, 0, 1)
-        w_group(0, "vector")
-        x_turn(0, 1, 0, "vector")
-        x_turn(0, 1, 1, "scalar")
-        w_quant(0)
-        w_group(1, "vector")
-        g_mult(0, 0, 1)
-        x_quant(0, 1, 0)
-        x_quant(0, 1, 1)
-        w_quant(1)
-        x_turn(1, 0, 0, "scalar")
-        x_turn(1, 0, 1, "scalar")
-        g_quant(0, 0, 0)
-        a_half(0, 0)
-        a_half(1, 0)
-        g_quant(0, 0, 1)
-        x_quant(1, 0, 0)
-        lc_sign(1)
-        x_quant(1, 0, 1)
-        x_turn(1, 1, 0, "scalar")
-        x_turn(1, 1, 1, "scalar")
-        a_scale(0, 0)
-        x_quant(1, 1, 0)
-        a_scale(1, 0)
-        x_quant(1, 1, 1)
-        lc_turn(1, 0, "scalar")
-        lc_turn(1, 1, "scalar")
-        w_group(2, "vector")
 
-        def live(i):
-            return 0 <= i < TILES
+        def halves(q):
+            return [(i, h) for i in (2 * q, 2 * q + 1) for h in range(2)]
 
-        g_rest = [(1, 0, 0), (1, 0, 1), (0, 1, 0), (0, 1, 1), (1, 1, 0), (1, 1, 1)]
-        g_plan = {0: g_rest[0:1], 1: g_rest[1:2], 2: g_rest[2:4], 3: g_rest[4:6]}
+        def update(q, engines):
+            for (i, h), engine in zip(halves(q), engines):
+                y_half(i, h)
+                y_step(i, h)
+                if engine == "gpsimd":
+                    y_round(i, h, engine)
+                if h == 1:
+                    y_store(i)
 
-        for n in range(TILES + LAG - 1):
-            j = n - LAG
-            unit = n + 3
-            if live(n):
-                if n > 1:
-                    a_half(n, 0)
-                a_half(n, 1)
-            if live(j):
-                y_mult(j)
-            if live(n - 2):
-                a_relu(n - 2)
-            if live(j - 3):
-                y_group(j - 3, "scalar" if n < TILES + 9 else "vector")
-            if live(j - 1):
-                y_round(j - 1)
-            if n == 0:
-                lc_quant(1, 0)
-                lc_quant(1, 1)
-            if n == 1:
-                wu_quant(1, 0)
-                wu_quant(1, 1)
-            if 2 < unit < TILES:
-                w_group(unit, "scalar" if unit in W_ON_SCALAR else "vector")
-            if live(n):
-                if n > 1:
-                    a_scale(n, 0)
-                a_scale(n, 1)
-            for quarter in g_plan.get(n - 1, []):
-                g_quant(*quarter)
-            for quarter in g_plan.get(n, []):
-                g_mult(*quarter)
-            if unit - 1 < TILES:
-                w_quant(unit - 1)
-            if live(n - 2):
-                a_quant(n - 2)
-            if live(j):
-                y_step(j, 0)
-            if live(j - 3):
-                y_quant(j - 3)
-            if live(j):
-                y_step(j, 1)
-                y_store(j)
-            if live(n - 1):
-                a_turn(n - 1)
-            if live(j - 2):
-                y_turn(j - 2)
-            if n == 0:
-                wu_turn(1, 0, "scalar")
-                wu_turn(1, 1, "scalar")
+        def y_planes(q):
+            y_quant(2 * q, 2, 0)
+            y_quant(2 * q, 2, 1)
 
-        last = TILES - 1
-        y_mult(last)
-        y_round(last - 1)
-        y_group(last - 3, "vector")
-        y_step(last, 0)
-        y_turn(last - 2)
-        y_quant(last - 3)
-        y_step(last, 1)
-        y_store(last)
-        y_finish_round(last, 0, "scalar")
-        y_turn(last - 1)
-        y_group(last - 2, "vector")
-        y_finish_round(last, 1, "scalar")
-        y_quant(last - 2)
-        y_group(last - 1, "vector")
-        y_finish_turn(last, 0, "scalar")
-        y_finish_turn(last, 1, "scalar")
-        y_quant(last - 1)
-        y_quant(last, (0,))
-        y_quant(last, (1,))
+        with tc.manual_schedule(engines={mybir.EngineType.PE}):
+            VE, SC = "vector", "scalar"
+            weight_prepare()
+            weight_spread(0)
+            weight_spread(1)
+            lc_sign(0)
+            for a in range(2):
+                lc_turn(0, a)
+                lc_group(0, a, SC)
+            for a in range(2):
+                wu_sort(0, a, VE)
+            for c in range(2):
+                x_sort(0, 0, c, VE)
+            lc_quant(0)
+            for a in range(2):
+                wu_turn(0, a)
+                wu_group(0, a, (SC, VE)[a])
+            wu_quant(0, 0)
+            for c in range(2):
+                x_turn(0, 0, c)
+                x_sort(0, 1, c, VE)
+                x_group(0, 0, c, SC)
+            wu_quant(0, 1)
+            rows_turn()
+            for n in range(2):
+                g_mult(0, 0, n)
+                g_group(0, 0, n, SC)
+                w_group(0, n, VE)
+            for c in range(2):
+                x_turn(0, 1, c)
+                x_group(0, 1, c, SC)
+            w_quant(0)
+            x_quant(0, 0)
+            x_quant(0, 1)
+            for c in range(2):
+                x_turn(1, 0, c)
+            for n in range(2, 4):
+                g_mult(0, 0, n)
+            w_group(1, 0, SC)
+            for c in range(2):
+                x_group(1, 0, c, SC)
+            for n in range(2, 4):
+                g_group(0, 0, n, (VE, SC)[n - 2])
+            lc_sign(1)
+            a_half(0, 0)
+            a_half(1, 0)
+            w_group(1, 1, VE)
+            a_scale(0, 0)
+            w_quant(1)
+            a_scale(1, 0)
+            g_quant(0, 0)
+            for c in range(2):
+                x_turn(1, 1, c)
+                x_group(1, 1, c, SC)
+                x_quant(1, c)
+            for a in range(2):
+                lc_turn(1, a)
+                lc_group(1, a, SC)
+            a_half(2, 0)
+            a_half(3, 0)
+            a_scale(2, 0)
+            lc_quant(1)
+            a_scale(3, 0)
+            for a in range(2):
+                wu_turn(1, a)
+                wu_group(1, a, SC)
+            w_group(2, 0, SC)
+            for i in range(4):
+                a_half(i, 1)
+                g_mult(1, 0, i)
+                a_scale(i, 1)
+                g_group(1, 0, i, SC)
+                if i == 0:
+                    wu_quant(1)
+                if i == 0:
+                    w_group(2, 1, SC)
+                if i == 2:
+                    w_quant(2)
+                    w_group(3, 0, VE)
+            a_turn(0)
+            a_turn(1)
+            a_relu(0)
+            for g in range(2):
+                for n in range(4):
+                    g_mult(g, 1, n)
+                    g_group(g, 1, n, (VE, SC, SC, SC, VE, SC, VE, SC)[4 * g + n])
+                    if n % 2 == 1:
+                        a_half(4 + g, n // 2)
+                        a_scale(4 + g, n // 2)
+                    if n == 0:
+                        g_quant(1 - g, g)
+                if g == 0:
+                    a_relu(1)
+                    w_group(3, 1, VE)
+                    a_turn(2)
+                    a_turn(3)
+            a_quant(0)
+            g_quant(1, 1)
+            a_relu(2)
+            a_relu(3)
+            turn["head"] = 0
+            a_turn(4)
+            a_turn(5)
+            w_quant(3)
+
+        with tc.manual_schedule():
+            for s in range(LAG, PAIRS):
+                j = s - LAG
+                update(j, ["gpsimd"] * 4)
+                for i, g in halves(s):
+                    a_half(i, g)
+                    a_scale(i, g)
+                a_relu(2 * s - 2)
+                a_relu(2 * s - 1)
+                if j > 0:
+                    y_group(2 * j - 2, "scalar")
+                    y_group(2 * j - 1, "scalar")
+                if s + 1 < PAIRS:
+                    w_group(s + 1, 0, "scalar")
+                    w_group(s + 1, 1, "scalar")
+                if s == LAG:
+                    a_quant(s - 2)
+                a_quant(s - 1)
+                if j > 0:
+                    y_planes(j - 1)
+                if s + 1 < PAIRS:
+                    w_quant(s + 1)
+                y_turn(2 * j)
+                a_turn(2 * s)
+                y_turn(2 * j + 1)
+                a_turn(2 * s + 1)
+
+            last = PAIRS - 1
+            a_relu(2 * last)
+            a_relu(2 * last + 1)
+            y_group(2 * last - 6, "scalar")
+            y_group(2 * last - 5, "scalar")
+            update(last - 2, ["gpsimd", "gpsimd", "scalar", "scalar"])
+            y_round(2 * last - 3, 0, "scalar")
+            y_round(2 * last - 3, 1, "scalar")
+            a_quant(last)
+            y_planes(last - 3)
+            update(last - 1, ["gpsimd"] * 4)
+            y_turn(2 * last - 4)
+            y_turn(2 * last - 3)
+            y_group(2 * last - 4, "scalar")
+            y_group(2 * last - 3, "scalar")
+            update(last, ["scalar"] * 4)
+            y_round(2 * last, 0, "scalar")
+            y_round(2 * last, 1, "scalar")
+            y_round(2 * last + 1, 0, "scalar")
+            y_planes(last - 2)
+            y_round(2 * last + 1, 1, "vector")
+            y_turn(2 * last - 2)
+            y_turn(2 * last - 1)
+            y_turn(2 * last)
+            y_turn(2 * last + 1)
+            y_group(2 * last - 2, "scalar")
+            y_group(2 * last - 1, "vector")
+            y_group(2 * last, "scalar")
+            y_group(2 * last + 1, "vector")
+            y_planes(last - 1)
+            y_planes(last)

@@ -20,7 +20,7 @@ KP = 512
 TILES = F // P
 PAIRS = TILES // 2
 LAG = 3
-WORD_BATCHES = ((0, 4), (4, 8), (8, 12), (12, 14), (14, 16))
+WORD_BATCHES = ((0, 4), (4, 8), (8, 10), (10, 12), (12, 14), (14, 16))
 SCALE_BATCHES = ((0, 10), (10, 16))
 MX_BANKS = (0, 1, 2, 3)
 TR_BANKS = (4, 5, 6, 7)
@@ -35,6 +35,7 @@ def tile_sae_decoder_logit_step_h3_kernel(
         keep = ctx.enter_context(tc.tile_pool(name="keep", bufs=1))
         work = ctx.enter_context(tc.tile_pool(name="work", bufs=3))
         psum = ctx.enter_context(tc.psum_pool(name="psum", bufs=1))
+        ctx.enter_context(tc.manual_schedule())
 
         turn = {"mx": 0, "tr": 0, "any": 0, "head": 1}
 
@@ -70,6 +71,7 @@ def tile_sae_decoder_logit_step_h3_kernel(
             )
 
         tw_raw = keep.tile([P, 2, 4], BF16, name="tw_raw")
+        nc.sync.dma_start(out=tw_raw[:], in_=token_weight.rearrange("(g p j) -> p g j", g=2, j=4))
         rows_raw = keep.tile([32, P], BF16, name="rows_raw")
         nc.scalar.dma_start(out=rows_raw[0:TILES, :], in_=b_enc.rearrange("(i p) -> i p", p=P))
         nc.scalar.dma_start(out=rows_raw[TILES : 2 * TILES, :], in_=step.rearrange("(i p) -> i p", p=P))
@@ -102,23 +104,21 @@ def tile_sae_decoder_logit_step_h3_kernel(
             rows = w_dec[2 * P * q : 2 * P * (q + 1), :]
             nc.sync.dma_start(out=wd_raw[q][:], in_=rows.rearrange("(a p) d -> p a d", a=2))
 
-        with tc.manual_schedule(engines={mybir.EngineType.SP}):
-            nc.sync.dma_start(out=tw_raw[:], in_=token_weight.rearrange("(g p j) -> p g j", g=2, j=4))
-            load_lc(0)
-            load_wu(0)
-            load_x(0, 0)
-            load_x(0, 1)
-            load_w(0)
-            load_x(1, 0)
-            load_x(1, 1)
-            load_lc(1)
-            load_wu(1)
-            load_w(1)
-            load_wd(0)
-            load_w(2)
-            load_wd(1)
-            load_w(3)
-            load_wd(2)
+        load_lc(0)
+        load_wu(0)
+        load_x(0, 0)
+        load_x(0, 1)
+        load_w(0)
+        load_x(1, 0)
+        load_x(1, 1)
+        load_lc(1)
+        load_wu(1)
+        load_w(1)
+        load_wd(0)
+        load_w(2)
+        load_wd(1)
+        load_w(3)
+        load_wd(2)
 
         ident = keep.tile([P, P], F32, name="ident")
         make_identity(nc, ident[:])
@@ -359,29 +359,31 @@ def tile_sae_decoder_logit_step_h3_kernel(
             else:
                 copy_on(engine, out, in_)
 
-        def y_turn(i, groups=(0, 1)):
+        def y_turn(q, g):
             turned = bank("tr")
-            for g in groups:
-                staged["yturned", i, g] = turned
-                words = staged["yr", i, g][:].bitcast(F32)
+            staged["yturned", q, g] = turned
+            for a in range(2):
+                words = staged["yr", 2 * q + a, g][:].bitcast(F32)
                 for u in range(2):
-                    first = 256 * g + P * u
+                    first = 256 * a + P * u
                     nc.tensor.transpose(turned[:, first : first + P], words[:, P * u : P * (u + 1)], ident[:])
 
-        def y_group(i, engine, groups=(0, 1)):
-            if ("yg", i // 2) not in staged:
-                staged["yg", i // 2] = work.tile([P, 2048], BF16, name="y_grouped", bufs=3, align_bytes=64)
-            span = slice(groups[0], groups[-1] + 1)
-            words = staged["yg", i // 2][:].bitcast(F32).rearrange("p (g a m u) -> p g a m u", g=2, a=2, u=2)
-            turned = staged["yturned", i, groups[0]][:].rearrange("p (g u m) -> p g m u", g=2, u=2)
-            copy_on(engine, words[:, span, i % 2, :, :], turned[:, span, :, :])
+        def y_group(q, g, engine):
+            grouped = work.tile([P, 1024], BF16, name="y_grouped", bufs=4, align_bytes=64)
+            staged["yg", q, g] = grouped
+            copy_on(
+                engine,
+                grouped[:].bitcast(F32).rearrange("p (a m u) -> p a m u", a=2, u=2),
+                staged["yturned", q, g][:].rearrange("p (a u m) -> p a m u", a=2, u=2),
+            )
 
         words_out = out_1.rearrange("g p m t -> p g (m t)").bitcast(I32)
         scales_out = out_2.rearrange("g q m -> q g m").bitcast(I32)
         word_batch = {i: (first, last) for first, last in WORD_BATCHES for i in range(first, last)}
         scale_batch = {i: (first, last) for first, last in SCALE_BATCHES for i in range(first, last)}
 
-        def y_quant(first, count, g):
+        def y_quant(q, g):
+            first, count = 2 * q, 2
             w_first, w_last = word_batch[first]
             s_first, s_last = scale_batch[first]
             if ("ycodes", w_first) not in staged:
@@ -394,11 +396,10 @@ def tile_sae_decoder_logit_step_h3_kernel(
                 )
             codes, scales = staged["ycodes", w_first], staged["yscales", s_first]
             end = first + count
-            start = 1024 * g + KP * (first % 2)
             nc.vector.quantize_mx(
                 out=codes[:, g, P * (first - w_first) : P * (end - w_first)].bitcast(FP8X4),
                 scales=scales[:, g, P * (first - s_first) : P * (end - s_first)],
-                in_=staged["yg", first // 2][:, start : start + KP * count],
+                in_=staged["yg", q, g][:],
             )
             if end == w_last and g == 1:
                 nc.sync.dma_start(out=words_out[:, :, P * w_first : P * w_last], in_=codes[:].bitcast(I32))
@@ -409,6 +410,115 @@ def tile_sae_decoder_logit_step_h3_kernel(
                         in_=scales[32 * quad : 32 * quad + 4, :, :].bitcast(I32),
                     )
 
+        VE, SC = "vector", "scalar"
+        weight_prepare()
+        weight_spread(0)
+        weight_spread(1)
+        lc_sign(0)
+        for a in range(2):
+            lc_turn(0, a)
+            lc_group(0, a, SC)
+        for a in range(2):
+            wu_sort(0, a, VE)
+        for c in range(2):
+            x_sort(0, 0, c, VE)
+        lc_quant(0)
+        for a in range(2):
+            wu_turn(0, a)
+            wu_group(0, a, SC)
+        wu_quant(0, 0)
+        for c in range(2):
+            x_turn(0, 0, c)
+            x_group(0, 0, c, SC)
+        wu_quant(0, 1)
+        rows_turn()
+        w_group(1, 0, SC)
+        w_group(0, 0, VE)
+        w_group(0, 1, VE)
+        w_group(1, 1, VE)
+        for n in range(2):
+            g_mult(0, 0, n)
+            g_group(0, 0, n, SC)
+        for u in (1, 0):
+            for c in range(2):
+                x_turn(1 - u, u, c)
+                x_group(1 - u, u, c, SC)
+        w_quant(0)
+        x_quant(0, 0)
+        x_quant(0, 1)
+        w_quant(1)
+        for n in range(2, 4):
+            g_mult(0, 0, n)
+            g_group(0, 0, n, SC)
+
+        lc_sign(1)
+        for i in range(2):
+            a_half(i, 0)
+            a_scale(i, 0)
+        g_quant(0, 0)
+        w_group(2, 0, SC)
+        w_group(3, 0, VE)
+        w_group(2, 1, VE)
+        for c in range(2):
+            x_turn(1, 1, c)
+            x_group(1, 1, c, SC)
+            x_quant(1, c)
+        for a in range(2):
+            lc_turn(1, a)
+            lc_group(1, a, SC)
+        w_group(3, 1, SC)
+        a_half(2, 0)
+        a_half(3, 0)
+        a_scale(2, 0)
+        lc_quant(1)
+        a_scale(3, 0)
+        for a in range(2):
+            wu_turn(1, a)
+            wu_group(1, a, SC)
+        for i in range(4):
+            a_half(i, 1)
+            g_mult(1, 0, i)
+            a_scale(i, 1)
+            g_group(1, 0, i, SC)
+            if i == 0:
+                w_quant(2)
+                wu_quant(1)
+        w_quant(3)
+        a_turn(0)
+        a_turn(1)
+        a_relu(0)
+        for n in range(4):
+            g_mult(0, 1, n)
+            if n == 1:
+                a_half(4, 0)
+        g_quant(1, 0)
+        g_group(0, 1, 0, VE)
+        g_group(0, 1, 1, SC)
+        a_relu(1)
+        a_scale(4, 0)
+        g_group(0, 1, 2, VE)
+        g_group(0, 1, 3, SC)
+        for n in range(4):
+            g_mult(1, 1, n)
+            if n == 1:
+                a_half(4, 1)
+        g_group(1, 1, 0, SC)
+        g_group(1, 1, 1, SC)
+        a_scale(4, 1)
+        g_group(1, 1, 2, SC)
+        g_group(1, 1, 3, SC)
+        a_quant(0)
+        a_half(5, 0)
+        a_half(5, 1)
+        a_scale(5, 0)
+        a_scale(5, 1)
+        g_quant(0, 1)
+        g_quant(1, 1)
+        turn["head"] = 0
+        for i in range(2, 6):
+            a_turn(i)
+        a_relu(2)
+        a_relu(3)
 
         def halves(q):
             return [(i, h) for i in (2 * q, 2 * q + 1) for h in range(2)]
@@ -423,169 +533,60 @@ def tile_sae_decoder_logit_step_h3_kernel(
                     y_store(i)
 
         def y_planes(q):
-            y_quant(2 * q, 2, 0)
-            y_quant(2 * q, 2, 1)
+            y_quant(q, 0)
+            y_quant(q, 1)
 
-        with tc.manual_schedule(engines={mybir.EngineType.PE}):
-            VE, SC = "vector", "scalar"
-            weight_prepare()
-            weight_spread(0)
-            weight_spread(1)
-            lc_sign(0)
-            for a in range(2):
-                lc_turn(0, a)
-                lc_group(0, a, SC)
-            for a in range(2):
-                wu_sort(0, a, VE)
-            for c in range(2):
-                x_sort(0, 0, c, VE)
-            lc_quant(0)
-            for a in range(2):
-                wu_turn(0, a)
-                wu_group(0, a, (SC, VE)[a])
-            wu_quant(0, 0)
-            for c in range(2):
-                x_turn(0, 0, c)
-                x_sort(0, 1, c, VE)
-                x_group(0, 0, c, SC)
-            wu_quant(0, 1)
-            rows_turn()
-            for n in range(2):
-                g_mult(0, 0, n)
-                g_group(0, 0, n, SC)
-                w_group(0, n, VE)
-            for c in range(2):
-                x_turn(0, 1, c)
-                x_group(0, 1, c, SC)
-            w_quant(0)
-            x_quant(0, 0)
-            x_quant(0, 1)
-            for c in range(2):
-                x_turn(1, 0, c)
-            for n in range(2, 4):
-                g_mult(0, 0, n)
-            w_group(1, 0, SC)
-            for c in range(2):
-                x_group(1, 0, c, SC)
-            for n in range(2, 4):
-                g_group(0, 0, n, (VE, SC)[n - 2])
-            lc_sign(1)
-            a_half(0, 0)
-            a_half(1, 0)
-            w_group(1, 1, VE)
-            a_scale(0, 0)
-            w_quant(1)
-            a_scale(1, 0)
-            g_quant(0, 0)
-            for c in range(2):
-                x_turn(1, 1, c)
-                x_group(1, 1, c, SC)
-                x_quant(1, c)
-            for a in range(2):
-                lc_turn(1, a)
-                lc_group(1, a, SC)
-            a_half(2, 0)
-            a_half(3, 0)
-            a_scale(2, 0)
-            lc_quant(1)
-            a_scale(3, 0)
-            for a in range(2):
-                wu_turn(1, a)
-                wu_group(1, a, SC)
-            w_group(2, 0, SC)
-            for i in range(4):
-                a_half(i, 1)
-                g_mult(1, 0, i)
-                a_scale(i, 1)
-                g_group(1, 0, i, SC)
-                if i == 0:
-                    wu_quant(1)
-                if i == 0:
-                    w_group(2, 1, SC)
-                if i == 2:
-                    w_quant(2)
-                    w_group(3, 0, VE)
-            a_turn(0)
-            a_turn(1)
-            a_relu(0)
-            for g in range(2):
-                for n in range(4):
-                    g_mult(g, 1, n)
-                    g_group(g, 1, n, (VE, SC, SC, SC, VE, SC, VE, SC)[4 * g + n])
-                    if n % 2 == 1:
-                        a_half(4 + g, n // 2)
-                        a_scale(4 + g, n // 2)
-                    if n == 0:
-                        g_quant(1 - g, g)
-                if g == 0:
-                    a_relu(1)
-                    w_group(3, 1, VE)
-                    a_turn(2)
-                    a_turn(3)
-            a_quant(0)
-            g_quant(1, 1)
-            a_relu(2)
-            a_relu(3)
-            turn["head"] = 0
-            a_turn(4)
-            a_turn(5)
-            w_quant(3)
-
-        with tc.manual_schedule():
-            for s in range(LAG, PAIRS):
-                j = s - LAG
-                update(j, ["gpsimd"] * 4)
-                for i, g in halves(s):
+        for s in range(LAG, PAIRS):
+            j = s - LAG
+            update(j, ["gpsimd"] * 4)
+            for i in (2 * s, 2 * s + 1):
+                for g in range(2):
                     a_half(i, g)
                     a_scale(i, g)
-                a_relu(2 * s - 2)
-                a_relu(2 * s - 1)
-                if j > 0:
-                    y_group(2 * j - 2, "scalar")
-                    y_group(2 * j - 1, "scalar")
-                if s + 1 < PAIRS:
-                    w_group(s + 1, 0, "scalar")
-                    w_group(s + 1, 1, "scalar")
-                if s == LAG:
-                    a_quant(s - 2)
-                a_quant(s - 1)
-                if j > 0:
-                    y_planes(j - 1)
-                if s + 1 < PAIRS:
-                    w_quant(s + 1)
-                y_turn(2 * j)
-                a_turn(2 * s)
-                y_turn(2 * j + 1)
-                a_turn(2 * s + 1)
+            a_relu(2 * s - 2)
+            a_relu(2 * s - 1)
+            if j > 0:
+                y_group(j - 1, 0, "scalar")
+                y_group(j - 1, 1, "scalar")
+            if s + 1 < PAIRS:
+                w_group(s + 1, 0, "scalar")
+                w_group(s + 1, 1, "scalar")
+            if s == LAG:
+                a_quant(s - 2)
+            a_quant(s - 1)
+            if j > 0:
+                y_planes(j - 1)
+            if s + 1 < PAIRS:
+                w_quant(s + 1)
+            y_turn(j, 0)
+            a_turn(2 * s)
+            y_turn(j, 1)
+            a_turn(2 * s + 1)
 
-            last = PAIRS - 1
-            a_relu(2 * last)
-            a_relu(2 * last + 1)
-            y_group(2 * last - 6, "scalar")
-            y_group(2 * last - 5, "scalar")
-            update(last - 2, ["gpsimd", "gpsimd", "scalar", "scalar"])
-            y_round(2 * last - 3, 0, "scalar")
-            y_round(2 * last - 3, 1, "scalar")
-            a_quant(last)
-            y_planes(last - 3)
-            update(last - 1, ["gpsimd"] * 4)
-            y_turn(2 * last - 4)
-            y_turn(2 * last - 3)
-            y_group(2 * last - 4, "scalar")
-            y_group(2 * last - 3, "scalar")
-            update(last, ["scalar"] * 4)
-            y_round(2 * last, 0, "scalar")
-            y_round(2 * last, 1, "scalar")
-            y_round(2 * last + 1, 0, "scalar")
-            y_planes(last - 2)
-            y_round(2 * last + 1, 1, "vector")
-            y_turn(2 * last - 2)
-            y_turn(2 * last - 1)
-            y_turn(2 * last)
-            y_turn(2 * last + 1)
-            y_group(2 * last - 2, "scalar")
-            y_group(2 * last - 1, "vector")
-            y_group(2 * last, "scalar")
-            y_group(2 * last + 1, "vector")
-            y_planes(last - 1)
-            y_planes(last)
+        last = PAIRS - 1
+        a_relu(2 * last)
+        a_relu(2 * last + 1)
+        y_group(last - 3, 0, "scalar")
+        y_group(last - 3, 1, "scalar")
+        for q in (last - 2, last - 1):
+            update(q, ["gpsimd", "gpsimd", "scalar", "scalar"])
+            if q == last - 1:
+                for g in range(2):
+                    y_turn(q - 1, g)
+                    y_group(q - 1, g, "scalar")
+            for h in range(2):
+                y_round(2 * q + 1, h, "scalar")
+            if q == last - 2:
+                a_quant(last)
+                y_planes(last - 3)
+        update(last, ["gpsimd", "scalar", "scalar", "scalar"])
+        y_round(2 * last, 1, "scalar")
+        y_round(2 * last + 1, 0, "vector")
+        y_round(2 * last + 1, 1, "vector")
+        y_planes(last - 2)
+        for q in (last - 1, last):
+            for g in range(2):
+                y_turn(q, g)
+                y_group(q, g, "scalar")
+        y_planes(last - 1)
+        y_planes(last)

@@ -14,17 +14,17 @@ U8 = mybir.dt.uint8
 FP8X4 = mybir.dt.float8_e4m3fn_x4
 ALU = mybir.AluOpType
 ACT = mybir.ActivationFunctionType
+VECTOR, SCALAR, GPSIMD = "vector", "scalar", "gpsimd"
 
 P = 128
 KP = 512
+HALF = 256
 TILES = F // P
 PAIRS = TILES // 2
 LAG = 3
-WORD_BATCHES = ((0, 4), (4, 8), (8, 10), (10, 12), (12, 14), (14, 16))
-SCALE_BATCHES = ((0, 10), (10, 16))
-MX_BANKS = (0, 1, 2, 3)
-TR_BANKS = (4, 5, 6, 7)
-POOL_HALVES = 4
+CODE_STORES = ((0, 4), (4, 8), (8, 10), (10, 12), (12, 14), (14, 16))
+SCALE_STORES = ((0, 8), (8, 16))
+BANKS = {"product": (0, 1, 2, 3), "turn": (4, 5, 6, 7), "any": (0, 1, 2, 3, 4, 5, 6, 7)}
 
 
 def tile_sae_decoder_logit_step_h3_kernel(
@@ -37,27 +37,22 @@ def tile_sae_decoder_logit_step_h3_kernel(
         psum = ctx.enter_context(tc.psum_pool(name="psum", bufs=1))
         ctx.enter_context(tc.manual_schedule())
 
-        turn = {"mx": 0, "tr": 0, "any": 0, "head": 1}
+        banks_taken = {"product": 0, "turn": 0, "any": 0}
+        roles_fixed = []
+        tiles = {}
 
-        def bank(kind):
-            if turn["head"]:
-                kind = "any"
-            banks = {"mx": MX_BANKS, "tr": TR_BANKS, "any": MX_BANKS + TR_BANKS}[kind]
-            number = banks[turn[kind] % len(banks)]
-            turn[kind] = turn[kind] + 1
+        def bank(role):
+            role = role if roles_fixed else "any"
+            number = BANKS[role][banks_taken[role] % len(BANKS[role])]
+            banks_taken[role] = banks_taken[role] + 1
             return psum.tile([P, KP], F32, name="bank%d" % number)
 
-        def planes(name, width, pool=keep, bufs=None):
-            codes = pool.tile([P, width], U32, name=name + "_codes", align_bytes=64, bufs=bufs)
-            scales = pool.tile([P, width], U8, name=name + "_scales", align_bytes=64, bufs=bufs)
+        def mx_operand(name, pool=keep, bufs=None):
+            codes = pool.tile([P, KP], U32, name=name + "_codes", align_bytes=64, bufs=bufs)
+            scales = pool.tile([P, KP], U8, name=name + "_scales", align_bytes=64, bufs=bufs)
             return codes, scales
 
-        def quantize(dst, first, src):
-            codes, scales = dst
-            cols = slice(first, first + src.shape[1] // 4)
-            nc.vector.quantize_mx(out=codes[:, cols].bitcast(FP8X4), scales=scales[:, cols], in_=src)
-
-        def mx(out, stationary, s_first, moving, m_first, width, start, stop):
+        def multiply(out, stationary, s_first, moving, m_first, width, start, stop):
             s_cols = slice(s_first, s_first + P)
             m_cols = slice(m_first, m_first + width)
             nc.tensor.matmul_mx(
@@ -70,9 +65,15 @@ def tile_sae_decoder_logit_step_h3_kernel(
                 stop=stop,
             )
 
+        def copy_on(engine, out, in_):
+            if engine == SCALAR:
+                nc.scalar.copy(out=out, in_=in_)
+            else:
+                nc.vector.tensor_copy(out=out, in_=in_)
+
         tw_raw = keep.tile([P, 2, 4], BF16, name="tw_raw")
-        nc.sync.dma_start(out=tw_raw[:], in_=token_weight.rearrange("(g p j) -> p g j", g=2, j=4))
-        rows_raw = keep.tile([32, P], BF16, name="rows_raw")
+        nc.sync.dma_start(out=tw_raw[:], in_=token_weight.rearrange("(g p t) -> p g t", g=2, t=4))
+        rows_raw = keep.tile([2 * TILES, P], BF16, name="rows_raw")
         nc.scalar.dma_start(out=rows_raw[0:TILES, :], in_=b_enc.rearrange("(i p) -> i p", p=P))
         nc.scalar.dma_start(out=rows_raw[TILES : 2 * TILES, :], in_=step.rearrange("(i p) -> i p", p=P))
 
@@ -83,25 +84,25 @@ def tile_sae_decoder_logit_step_h3_kernel(
             rows = x[KP * g : KP * (g + 1), :].rearrange("(p u e) d -> p u e d", u=2, e=2)
             nc.sync.dma_start(out=x_raw[g, u][:], in_=rows[:, u, :, :])
 
-        def load_w(k):
+        def load_w(chunk):
             for c in range(2):
-                w_raw[k, c] = keep.tile([P, 4, KP], BF16, name="w_raw%d%d" % (k, c))
-                rows = w_enc[KP * c : KP * (c + 1), KP * k : KP * (k + 1)]
-                nc.sync.dma_start(out=w_raw[k, c][:], in_=rows.rearrange("(p j) f -> p j f", j=4))
+                w_raw[chunk, c] = keep.tile([P, 4, KP], BF16, name="w_raw%d%d" % (chunk, c))
+                rows = w_enc[KP * c : KP * (c + 1), KP * chunk : KP * (chunk + 1)]
+                nc.sync.dma_start(out=w_raw[chunk, c][:], in_=rows.rearrange("(p t) f -> p t f", t=4))
 
         def load_lc(g):
             lc_raw[g] = keep.tile([P, 4, V], BF16, name="lc_raw%d" % g)
             rows = logit_cotangent[KP * g : KP * (g + 1), :]
-            nc.sync.dma_start(out=lc_raw[g][:], in_=rows.rearrange("(p j) v -> p j v", j=4))
+            nc.sync.dma_start(out=lc_raw[g][:], in_=rows.rearrange("(p t) v -> p t v", t=4))
 
         def load_wu(h):
             wu_raw[h] = keep.tile([P, 2, 2, V], BF16, name="wu_raw%d" % h)
             rows = w_unembed[KP * h : KP * (h + 1), :]
-            nc.sync.dma_start(out=wu_raw[h][:], in_=rows.rearrange("(a p j) v -> p a j v", a=2, j=2))
+            nc.sync.dma_start(out=wu_raw[h][:], in_=rows.rearrange("(a p e) v -> p a e v", a=2, e=2))
 
         def load_wd(q):
-            wd_raw[q] = work.tile([P, 2, D], BF16, name="wd_raw", bufs=3)
-            rows = w_dec[2 * P * q : 2 * P * (q + 1), :]
+            wd_raw[q] = work.tile([P, 2, D], BF16, name="wd_raw", bufs=LAG)
+            rows = w_dec[HALF * q : HALF * (q + 1), :]
             nc.sync.dma_start(out=wd_raw[q][:], in_=rows.rearrange("(a p) d -> p a d", a=2))
 
         load_lc(0)
@@ -113,12 +114,9 @@ def tile_sae_decoder_logit_step_h3_kernel(
         load_x(1, 1)
         load_lc(1)
         load_wu(1)
-        load_w(1)
-        load_wd(0)
-        load_w(2)
-        load_wd(1)
-        load_w(3)
-        load_wd(2)
+        for chunk in range(1, 4):
+            load_w(chunk)
+            load_wd(chunk - 1)
 
         ident = keep.tile([P, P], F32, name="ident")
         make_identity(nc, ident[:])
@@ -130,463 +128,428 @@ def tile_sae_decoder_logit_step_h3_kernel(
         minus_step = keep.tile([P, TILES], F32, name="minus_step")
         tw_abs = keep.tile([P, T], BF16, name="tw_abs")
 
-        def weight_prepare():
+        def widen_vectors():
+            weights = tw_raw[:].rearrange("p g t -> p (g t)")
             nc.vector.tensor_scalar(
-                out=half_sign[:], in0=tw_raw[:].rearrange("p g j -> p (g j)"), scalar1=0.0, scalar2=0.5,
-                op0=ALU.is_ge, op1=ALU.subtract,
+                out=half_sign[:], in0=weights, scalar1=0.0, scalar2=0.5, op0=ALU.is_ge, op1=ALU.subtract
             )
-            nc.vector.tensor_copy(out=tw32[:], in_=tw_raw[:].rearrange("p g j -> p (g j)"))
+            nc.vector.tensor_copy(out=tw32[:], in_=weights)
+            nc.vector.tensor_copy(out=rows32[0 : 2 * TILES, :], in_=rows_raw[:])
 
-            nc.vector.tensor_copy(out=rows32[0:32, :], in_=rows_raw[:])
-
-        def weight_spread(g):
-            spread = bank("mx")
-            for j in range(4):
-                column = tw32[:, 4 * g + j : 4 * g + j + 1].to_broadcast([P, P])
-                nc.tensor.transpose(spread[:, P * j : P * (j + 1)], column, ident[:])
+        def spread_weights(g):
+            spread = bank("product")
+            for t in range(4):
+                column = tw32[:, 4 * g + t : 4 * g + t + 1].to_broadcast([P, P])
+                nc.tensor.transpose(spread[:, P * t : P * (t + 1)], column, ident[:])
             nc.scalar.activation(
                 out=tw_abs[:, KP * g : KP * (g + 1)].rearrange("m (u p e) -> m u p e", u=2, e=2),
                 in_=spread[:].rearrange("m (u e p) -> m u p e", u=2, e=2),
                 func=ACT.Abs,
             )
 
-        def rows_turn():
-            turned = bank("mx")
+        def turn_vectors():
+            turned = bank("product")
             nc.tensor.transpose(turned[:, 0:P], rows32[:], ident[:])
             nc.vector.tensor_copy(out=bias[:], in_=turned[:, 0:TILES])
             nc.vector.tensor_scalar(
                 out=minus_step[:], in0=turned[:, TILES : 2 * TILES], scalar1=-1.0, scalar2=None, op0=ALU.mult
             )
 
-        def staging(key, half):
-            if key not in staged:
-                staged[key] = work.tile([P, 2048], BF16, name="grouped", bufs=5, align_bytes=64)
-            return staged[key][:, 1024 * half : 1024 * (half + 1)]
+        def grouped_half(key, half):
+            if key not in tiles:
+                tiles[key] = work.tile([P, 4 * KP], BF16, name="grouped", bufs=5, align_bytes=64)
+            return tiles[key][:, 4 * HALF * half : 4 * HALF * (half + 1)]
 
-        def quant(key, dst, half=None):
-            if half is None:
-                quantize(dst, 0, staged[key][:])
-            else:
-                quantize(dst, 256 * half, staged[key][:, 1024 * half : 1024 * (half + 1)])
+        def quantize(key, operand, halves=(0, 1)):
+            codes, scales = operand
+            first, end = HALF * halves[0], HALF * (halves[-1] + 1)
+            nc.vector.quantize_mx(
+                out=codes[:, first:end].bitcast(FP8X4),
+                scales=scales[:, first:end],
+                in_=tiles[key][:, 4 * first : 4 * end],
+            )
 
-        def turn_rows(sources, name, engine, kind="tr"):
-            turned = bank(kind)
+        def turn_four(sources):
+            turned = bank("turn")
             for n in range(4):
                 nc.tensor.transpose(turned[:, P * n : P * (n + 1)], sources[n], ident[:])
             return turned
 
-        x_q = {(g, c): planes("x%d%d" % (g, c), KP) for g in range(2) for c in range(2)}
-        lc_q = {g: planes("lc%d" % g, KP) for g in range(2)}
-        wu_q = {h: planes("wu%d" % h, KP) for h in range(2)}
-        g_q = {(g, h): planes("g%d%d" % (g, h), KP) for g in range(2) for h in range(2)}
-        w_q, a_q, staged = {}, {}, {}
-
-        def copy_on(engine, out, in_):
-            if engine == "scalar":
-                nc.scalar.copy(out=out, in_=in_)
-            else:
-                nc.vector.tensor_copy(out=out, in_=in_)
-
-        def x_turn(g, u, c):
-            if ("xs", g, u, c) in staged:
-                words = staged["xs", g, u, c]
-                sources = [words[:, P * n : P * (n + 1)] for n in range(4)]
-            else:
-                words = x_raw[g, u][:].bitcast(F32)
-                sources = [words[:, e, 256 * c + w : 256 * (c + 1) : 2] for e in range(2) for w in range(2)]
-            staged["xt", g, u, c] = turn_rows(sources, "x", "scalar")
-
-        def x_group(g, u, c, engine):
-            copy_on(
-                engine,
-                staging(("x", g, c), u).bitcast(F32).rearrange("k (p e w) -> k p e w", e=2, w=2),
-                staged["xt", g, u, c][:].rearrange("k (e w p) -> k p e w", e=2, w=2),
+        def sort_pairs(key, words):
+            ordered = work.tile([P, KP], F32, name="ordered", bufs=4)
+            tiles["sorted", key] = ordered
+            nc.vector.tensor_copy(
+                out=ordered[:].rearrange("k (e w p) -> k e w p", e=2, w=2),
+                in_=words.rearrange("k e (p w) -> k e w p", w=2),
             )
 
-        def x_sort(g, u, c, engine):
-            ordered = work.tile([P, KP], F32, name="ordered", bufs=4)
-            staged["xs", g, u, c] = ordered
-            words = x_raw[g, u][:].bitcast(F32)[:, :, 256 * c : 256 * (c + 1)]
-            copy_on(engine, ordered[:].rearrange("k (e w p) -> k e w p", e=2, w=2), words.rearrange("k e (p w) -> k e w p", w=2))
+        def turn_two_rows(key, words):
+            if ("sorted", key) in tiles:
+                sources = [tiles["sorted", key][:, P * n : P * (n + 1)] for n in range(4)]
+            else:
+                sources = [words[:, e, w:HALF:2] for e in range(2) for w in range(2)]
+            tiles["turned", key] = turn_four(sources)
 
-        def wu_sort(h, a, engine):
-            ordered = work.tile([P, KP], F32, name="ordered", bufs=4)
-            staged["wus", h, a] = ordered
-            words = wu_raw[h][:].bitcast(F32)[:, a, :, :]
-            copy_on(engine, ordered[:].rearrange("k (e w p) -> k e w p", e=2, w=2), words.rearrange("k e (p w) -> k e w p", w=2))
+        def group_two_rows(key, target):
+            nc.scalar.copy(
+                out=target.bitcast(F32).rearrange("k (p e w) -> k p e w", e=2, w=2),
+                in_=tiles["turned", key][:].rearrange("k (e w p) -> k p e w", e=2, w=2),
+            )
 
-        def x_quant(g, c, u=None):
-            quant(("x", g, c), x_q[g, c], u)
+        x_q = {(g, c): mx_operand("x%d%d" % (g, c)) for g in range(2) for c in range(2)}
+        lc_q = {g: mx_operand("lc%d" % g) for g in range(2)}
+        wu_q = {h: mx_operand("wu%d" % h) for h in range(2)}
+        g_q = {(g, h): mx_operand("g%d%d" % (g, h)) for g in range(2) for h in range(2)}
+        w_q, a_q = {}, {}
+
+        def x_words(g, u, c):
+            return x_raw[g, u][:].bitcast(F32)[:, :, HALF * c : HALF * (c + 1)]
+
+        def x_sort(g, u, c):
+            sort_pairs(("x", g, u, c), x_words(g, u, c))
+
+        def x_turn(g, u, c):
+            turn_two_rows(("x", g, u, c), x_words(g, u, c))
+
+        def x_group(g, u, c):
+            group_two_rows(("x", g, u, c), grouped_half(("x", g, c), u))
+
+        def x_quant(g, c):
+            quantize(("x", g, c), x_q[g, c])
 
         def lc_sign(g):
             signed = work.tile([P, 4, V], BF16, name="signed", bufs=1)
-            staged["signed", g] = signed
-            for j in range(4):
+            tiles["signed", g] = signed
+            for t in range(4):
                 nc.vector.tensor_scalar(
-                    out=signed[:, j, :].rearrange("p (w c e) -> p w c e", w=2, e=2),
-                    in0=lc_raw[g][:, j, :].rearrange("p (c w e) -> p w c e", w=2, e=2),
-                    scalar1=half_sign[:, 4 * g + j : 4 * g + j + 1], scalar2=2.0, op0=ALU.mult, op1=ALU.mult,
+                    out=signed[:, t, :].rearrange("p (w c e) -> p w c e", w=2, e=2),
+                    in0=lc_raw[g][:, t, :].rearrange("p (c w e) -> p w c e", w=2, e=2),
+                    scalar1=half_sign[:, 4 * g + t : 4 * g + t + 1],
+                    scalar2=2.0,
+                    op0=ALU.mult,
+                    op1=ALU.mult,
                 )
 
         def lc_turn(g, a):
-            words = staged["signed", g][:].rearrange("p j v -> p (j v)").bitcast(F32)
-            staged["lt", g, a] = turn_rows([words[:, P * n : P * (n + 1)] for n in range(4 * a, 4 * a + 4)], "lc", "scalar")
-
-        def lc_group(g, a, engine):
-            copy_on(
-                engine,
-                staging(("lc", g), a).bitcast(F32).rearrange("k (j p w) -> k j p w", j=2, w=2),
-                staged["lt", g, a][:].rearrange("k (j w p) -> k j p w", j=2, w=2),
+            words = tiles["signed", g][:].rearrange("p t v -> p (t v)").bitcast(F32)
+            turned = turn_four([words[:, P * n : P * (n + 1)] for n in range(4 * a, 4 * a + 4)])
+            nc.scalar.copy(
+                out=grouped_half(("lc", g), a).bitcast(F32).rearrange("k (j p w) -> k j p w", j=2, w=2),
+                in_=turned[:].rearrange("k (j w p) -> k j p w", j=2, w=2),
             )
 
-        def lc_quant(g, a=None):
-            quant(("lc", g), lc_q[g], a)
+        def wu_words(h, a):
+            return wu_raw[h][:].bitcast(F32)[:, a, :, :]
 
         def wu_turn(h, a):
-            if ("wus", h, a) in staged:
-                words = staged["wus", h, a]
-                sources = [words[:, P * n : P * (n + 1)] for n in range(4)]
-            else:
-                words = wu_raw[h][:].bitcast(F32)
-                sources = [words[:, a, j, w:256:2] for j in range(2) for w in range(2)]
-            staged["ut", h, a] = turn_rows(sources, "wu", "scalar")
-
-        def wu_group(h, a, engine):
-            copy_on(
-                engine,
-                staging(("wu", h), a).bitcast(F32).rearrange("k (p j w) -> k p j w", j=2, w=2),
-                staged["ut", h, a][:].rearrange("k (j w p) -> k p j w", j=2, w=2),
-            )
-
-        def wu_quant(h, a=None):
-            quant(("wu", h), wu_q[h], a)
+            turn_two_rows(("wu", h, a), wu_words(h, a))
+            group_two_rows(("wu", h, a), grouped_half(("wu", h), a))
 
         def g_mult(g, h, n):
-            acc = bank("mx")
-            staged["gt", g, h, n] = acc
+            acc = bank("product")
+            tiles["g", g, h, n] = acc
             for t in range(4):
-                mx(acc[:, P * t : P * (t + 1)], lc_q[g], P * t, wu_q[h], P * n, P, True, True)
+                multiply(acc[:, P * t : P * (t + 1)], lc_q[g], P * t, wu_q[h], P * n, P, True, True)
 
         def g_group(g, h, n, engine):
-            grouped = staging(("g", g, h), n // 2)
+            target = grouped_half(("g", g, h), n // 2)[:, KP * (n % 2) : KP * (n % 2 + 1)]
             copy_on(
                 engine,
-                grouped[:, KP * (n % 2) : KP * (n % 2 + 1)].rearrange("p (d t) -> p d t", t=4),
-                staged["gt", g, h, n][:].rearrange("p (t d) -> p d t", t=4),
+                target.rearrange("p (d t) -> p d t", t=4),
+                tiles["g", g, h, n][:].rearrange("p (t d) -> p d t", t=4),
             )
 
-        def g_quant(g, h, a=None):
-            quant(("g", g, h), g_q[g, h], a)
+        def g_quant(g, h):
+            quantize(("g", g, h), g_q[g, h])
 
         def w_group(q, c, engine):
             if c == 0:
-                staged["w", q] = work.tile([P, 2048], BF16, name="w_grouped", bufs=2, align_bytes=64)
-            cols = slice(256 * (q % 2), 256 * (q % 2 + 1))
+                tiles["w", q] = work.tile([P, 4 * KP], BF16, name="w_grouped", bufs=2, align_bytes=64)
+            cols = slice(HALF * (q % 2), HALF * (q % 2 + 1))
             copy_on(
                 engine,
-                staged["w", q][:, 1024 * c : 1024 * (c + 1)].rearrange("p (a i t) -> p a t i", i=4, t=4),
+                tiles["w", q][:, 4 * HALF * c : 4 * HALF * (c + 1)].rearrange("p (a i t) -> p a t i", i=4, t=4),
                 w_raw[q // 2, c][:, :, cols].rearrange("p t (a i) -> p a t i", i=4),
             )
 
-        def w_quant(q, c=None):
-            if q not in w_q:
-                w_q[q] = planes("w", KP, work, 3)
-            quant(("w", q), w_q[q], c)
+        def w_quant(q):
+            w_q[q] = mx_operand("w", work, 3)
+            quantize(("w", q), w_q[q])
 
-        def a_half(i, g):
-            acc = bank("mx")
-            staged["pre", i, g] = acc
+        def a_mult(i, g):
+            acc = bank("product")
+            tiles["pre", i, g] = acc
             for c in range(2):
-                mx(acc[:], w_q[i // 2], 256 * c + P * (i % 2), x_q[g, c], 0, KP, c == 0, c == 1)
+                multiply(acc[:], w_q[i // 2], HALF * c + P * (i % 2), x_q[g, c], 0, KP, c == 0, c == 1)
 
-        def a_scale(i, g):
+        def a_weigh(i, g):
             if g == 0:
-                staged["at", i] = work.tile([P, T], BF16, name="a_t", bufs=5)
+                tiles["weighed", i] = work.tile([P, T], BF16, name="a_t", bufs=5)
+            cols = slice(KP * g, KP * (g + 1))
             nc.vector.scalar_tensor_tensor(
-                out=staged["at", i][:, KP * g : KP * (g + 1)], in0=staged["pre", i, g][:], scalar=bias[:, i : i + 1],
-                in1=tw_abs[:, KP * g : KP * (g + 1)], op0=ALU.add, op1=ALU.mult,
+                out=tiles["weighed", i][:, cols],
+                in0=tiles["pre", i, g][:],
+                scalar=bias[:, i : i + 1],
+                in1=tw_abs[:, cols],
+                op0=ALU.add,
+                op1=ALU.mult,
             )
 
         def a_turn(i):
-            words = staged["at", i][:].bitcast(F32)
-            turned = turn_rows(
-                [words[:, 256 * g + P * u : 256 * g + P * (u + 1)] for u in range(2) for g in range(2)], "a", "scalar"
-            )
-            staged["aturned", i] = turned
+            words = tiles["weighed", i][:].bitcast(F32)
+            starts = [HALF * g + P * u for u in range(2) for g in range(2)]
+            tiles["a_turned", i] = turn_four([words[:, first : first + P] for first in starts])
 
         def a_relu(i):
-            if i % 2 == 0:
-                staged["a", i // 2] = work.tile([P, 2048], BF16, name="grouped", bufs=5, align_bytes=64)
-            grouped = staged["a", i // 2][:, 1024 * (i % 2) : 1024 * (i % 2 + 1)]
             nc.scalar.activation(
-                out=grouped[:].rearrange("p (m u e) -> p m u e", u=2, e=2),
-                in_=staged["aturned", i][:].bitcast(BF16).rearrange("p (u m e) -> p m u e", u=2, e=2),
+                out=grouped_half(("a", i // 2), i % 2).rearrange("p (m u e) -> p m u e", u=2, e=2),
+                in_=tiles["a_turned", i][:].bitcast(BF16).rearrange("p (u m e) -> p m u e", u=2, e=2),
                 func=ACT.Relu,
             )
 
-        def a_quant(q, half=None):
-            if q not in a_q:
-                a_q[q] = planes("a", KP, work, LAG + 1)
-            quant(("a", q), a_q[q], half)
+        def a_quant(q):
+            a_q[q] = mx_operand("a", work, LAG + 1)
+            quantize(("a", q), a_q[q])
 
-        def y_half(i, h):
-            acc = bank("mx")
-            staged["grad", i, h] = acc
+        def y_update(i, h):
+            acc = bank("product")
             for g in range(2):
-                mx(acc[:], a_q[i // 2], 256 * (i % 2) + P * g, g_q[g, h], 0, KP, g == 0, g == 1)
-
-        def y_step(i, h):
+                multiply(acc[:], a_q[i // 2], HALF * (i % 2) + P * g, g_q[g, h], 0, KP, g == 0, g == 1)
             if h == 0:
-                staged["y", i] = work.tile([P, D], F32, name="y", bufs=5)
+                tiles["y", i] = work.tile([P, D], F32, name="y", bufs=7)
             cols = slice(KP * h, KP * (h + 1))
             nc.vector.scalar_tensor_tensor(
-                out=staged["y", i][:, cols], in0=staged["grad", i, h][:], scalar=minus_step[:, i : i + 1],
-                in1=wd_raw[i // 2][:, i % 2, cols], op0=ALU.mult, op1=ALU.add,
+                out=tiles["y", i][:, cols],
+                in0=acc[:],
+                scalar=minus_step[:, i : i + 1],
+                in1=wd_raw[i // 2][:, i % 2, cols],
+                op0=ALU.mult,
+                op1=ALU.add,
             )
 
         def y_store(i):
-            nc.sync.dma_start(out=out_0[P * i : P * (i + 1), :], in_=staged["y", i][:])
-            if i % 2 == 1 and i // 2 + 3 < TILES // 2:
-                load_wd(i // 2 + 3)
+            nc.sync.dma_start(out=out_0[P * i : P * (i + 1), :], in_=tiles["y", i][:])
+            if i % 2 == 1 and i // 2 + LAG < PAIRS:
+                load_wd(i // 2 + LAG)
 
-        def y_round(i, g, engine):
+        def y_round(i, h, engine):
             rounded = work.tile([P, KP], BF16, name="y_rounded", bufs=8)
-            staged["yr", i, g] = rounded
+            tiles["rounded", i, h] = rounded
             out = rounded[:].rearrange("m (u c e) -> m u c e", u=2, e=2)
-            in_ = staged["y", i][:, KP * g : KP * (g + 1)].rearrange("m (c u e) -> m u c e", u=2, e=2)
-            if engine == "gpsimd":
+            in_ = tiles["y", i][:, KP * h : KP * (h + 1)].rearrange("m (c u e) -> m u c e", u=2, e=2)
+            if engine == GPSIMD:
                 nc.gpsimd.tensor_scalar(out=out, in0=in_, scalar1=1.0, scalar2=1.0, op0=ALU.mult, op1=ALU.mult)
             else:
                 copy_on(engine, out, in_)
 
-        def y_turn(q, g):
-            turned = bank("tr")
-            staged["yturned", q, g] = turned
-            for a in range(2):
-                words = staged["yr", 2 * q + a, g][:].bitcast(F32)
-                for u in range(2):
-                    first = 256 * a + P * u
-                    nc.tensor.transpose(turned[:, first : first + P], words[:, P * u : P * (u + 1)], ident[:])
+        def y_turn(q, h):
+            words = [tiles["rounded", 2 * q + a, h][:].bitcast(F32) for a in range(2)]
+            tiles["y_turned", q, h] = turn_four([words[a][:, P * u : P * (u + 1)] for a in range(2) for u in range(2)])
 
-        def y_group(q, g, engine):
-            grouped = work.tile([P, 1024], BF16, name="y_grouped", bufs=4, align_bytes=64)
-            staged["yg", q, g] = grouped
-            copy_on(
-                engine,
-                grouped[:].bitcast(F32).rearrange("p (a m u) -> p a m u", a=2, u=2),
-                staged["yturned", q, g][:].rearrange("p (a u m) -> p a m u", a=2, u=2),
+        def y_group(q, h):
+            grouped = work.tile([P, 4 * HALF], BF16, name="y_grouped", bufs=4, align_bytes=64)
+            tiles["y_grouped", q, h] = grouped
+            nc.scalar.copy(
+                out=grouped[:].bitcast(F32).rearrange("p (a m u) -> p a m u", a=2, u=2),
+                in_=tiles["y_turned", q, h][:].rearrange("p (a u m) -> p a m u", a=2, u=2),
             )
 
-        words_out = out_1.rearrange("g p m t -> p g (m t)").bitcast(I32)
-        scales_out = out_2.rearrange("g q m -> q g m").bitcast(I32)
-        word_batch = {i: (first, last) for first, last in WORD_BATCHES for i in range(first, last)}
-        scale_batch = {i: (first, last) for first, last in SCALE_BATCHES for i in range(first, last)}
+        codes_out = out_1.rearrange("g p m t -> p g (m t)").bitcast(I32)
+        scales_out = out_2.rearrange("g r m -> r g m").bitcast(I32)
+        code_store = {i: (first, end) for first, end in CODE_STORES for i in range(first, end)}
+        scale_store = {i: (first, end) for first, end in SCALE_STORES for i in range(first, end)}
 
-        def y_quant(q, g):
-            first, count = 2 * q, 2
-            w_first, w_last = word_batch[first]
-            s_first, s_last = scale_batch[first]
-            if ("ycodes", w_first) not in staged:
-                staged["ycodes", w_first] = work.tile(
-                    [P, 2, P * (w_last - w_first)], U32, name="y_codes", bufs=3, align_bytes=64
+        def y_planes(q):
+            first, end = 2 * q, 2 * q + 2
+            c_first, c_end = code_store[first]
+            s_first, s_end = scale_store[first]
+            if first == c_first:
+                width = P * (c_end - c_first)
+                tiles["y_codes"] = work.tile([P, 2, width], U32, name="y_codes", bufs=3, align_bytes=64)
+            if first == s_first:
+                width = P * (s_end - s_first)
+                tiles["y_scales"] = keep.tile([P, 2, width], U8, name="y_scales%d" % s_first, align_bytes=64)
+            codes, scales = tiles["y_codes"], tiles["y_scales"]
+            for h in range(2):
+                nc.vector.quantize_mx(
+                    out=codes[:, h, P * (first - c_first) : P * (end - c_first)].bitcast(FP8X4),
+                    scales=scales[:, h, P * (first - s_first) : P * (end - s_first)],
+                    in_=tiles["y_grouped", q, h][:],
                 )
-            if ("yscales", s_first) not in staged:
-                staged["yscales", s_first] = keep.tile(
-                    [P, 2, P * (s_last - s_first)], U8, name="y_scales%d" % s_first, align_bytes=64
-                )
-            codes, scales = staged["ycodes", w_first], staged["yscales", s_first]
-            end = first + count
-            nc.vector.quantize_mx(
-                out=codes[:, g, P * (first - w_first) : P * (end - w_first)].bitcast(FP8X4),
-                scales=scales[:, g, P * (first - s_first) : P * (end - s_first)],
-                in_=staged["yg", q, g][:],
-            )
-            if end == w_last and g == 1:
-                nc.sync.dma_start(out=words_out[:, :, P * w_first : P * w_last], in_=codes[:].bitcast(I32))
-            if end == s_last and g == 1:
+            if end == c_end:
+                nc.sync.dma_start(out=codes_out[:, :, P * c_first : P * c_end], in_=codes[:].bitcast(I32))
+            if end == s_end:
+                queue = nc.scalar if end == TILES else nc.sync
                 for quad in range(4):
-                    nc.sync.dma_start(
-                        out=scales_out[4 * quad : 4 * quad + 4, :, P * s_first // 4 : P * s_last // 4],
+                    queue.dma_start(
+                        out=scales_out[4 * quad : 4 * quad + 4, :, P * s_first // 4 : P * s_end // 4],
                         in_=scales[32 * quad : 32 * quad + 4, :, :].bitcast(I32),
                     )
 
-        VE, SC = "vector", "scalar"
-        weight_prepare()
-        weight_spread(0)
-        weight_spread(1)
+        widen_vectors()
+        spread_weights(0)
+        spread_weights(1)
         lc_sign(0)
+        lc_turn(0, 0)
+        lc_turn(0, 1)
         for a in range(2):
-            lc_turn(0, a)
-            lc_group(0, a, SC)
-        for a in range(2):
-            wu_sort(0, a, VE)
+            sort_pairs(("wu", 0, a), wu_words(0, a))
         for c in range(2):
-            x_sort(0, 0, c, VE)
-        lc_quant(0)
-        for a in range(2):
-            wu_turn(0, a)
-            wu_group(0, a, SC)
-        wu_quant(0, 0)
+            x_sort(0, 0, c)
+        quantize(("lc", 0), lc_q[0])
+        wu_turn(0, 0)
+        wu_turn(0, 1)
+        quantize(("wu", 0), wu_q[0], (0,))
         for c in range(2):
             x_turn(0, 0, c)
-            x_group(0, 0, c, SC)
-        wu_quant(0, 1)
-        rows_turn()
-        w_group(1, 0, SC)
-        w_group(0, 0, VE)
-        w_group(0, 1, VE)
-        w_group(1, 1, VE)
+            x_group(0, 0, c)
+        quantize(("wu", 0), wu_q[0], (1,))
+        turn_vectors()
+        w_group(1, 0, SCALAR)
+        w_group(0, 0, VECTOR)
+        w_group(0, 1, VECTOR)
+        w_group(1, 1, VECTOR)
         for n in range(2):
             g_mult(0, 0, n)
-            g_group(0, 0, n, SC)
-        for u in (1, 0):
+            g_group(0, 0, n, SCALAR)
+        for g, u in ((0, 1), (1, 0)):
             for c in range(2):
-                x_turn(1 - u, u, c)
-                x_group(1 - u, u, c, SC)
+                x_turn(g, u, c)
+                x_group(g, u, c)
         w_quant(0)
         x_quant(0, 0)
         x_quant(0, 1)
         w_quant(1)
         for n in range(2, 4):
             g_mult(0, 0, n)
-            g_group(0, 0, n, SC)
-
+            g_group(0, 0, n, SCALAR)
         lc_sign(1)
         for i in range(2):
-            a_half(i, 0)
-            a_scale(i, 0)
+            a_mult(i, 0)
+            a_weigh(i, 0)
         g_quant(0, 0)
-        w_group(2, 0, SC)
-        w_group(3, 0, VE)
-        w_group(2, 1, VE)
+        w_group(2, 0, SCALAR)
+        w_group(3, 0, VECTOR)
+        w_group(2, 1, VECTOR)
         for c in range(2):
             x_turn(1, 1, c)
-            x_group(1, 1, c, SC)
+            x_group(1, 1, c)
             x_quant(1, c)
-        for a in range(2):
-            lc_turn(1, a)
-            lc_group(1, a, SC)
-        w_group(3, 1, SC)
-        a_half(2, 0)
-        a_half(3, 0)
-        a_scale(2, 0)
-        lc_quant(1)
-        a_scale(3, 0)
-        for a in range(2):
-            wu_turn(1, a)
-            wu_group(1, a, SC)
+        lc_turn(1, 0)
+        lc_turn(1, 1)
+        w_group(3, 1, SCALAR)
+        a_mult(2, 0)
+        a_mult(3, 0)
+        a_weigh(2, 0)
+        quantize(("lc", 1), lc_q[1])
+        a_weigh(3, 0)
+        wu_turn(1, 0)
+        wu_turn(1, 1)
         for i in range(4):
-            a_half(i, 1)
+            a_mult(i, 1)
             g_mult(1, 0, i)
-            a_scale(i, 1)
-            g_group(1, 0, i, SC)
+            a_weigh(i, 1)
+            g_group(1, 0, i, SCALAR)
             if i == 0:
                 w_quant(2)
-                wu_quant(1)
+                quantize(("wu", 1), wu_q[1])
         w_quant(3)
         a_turn(0)
         a_turn(1)
         a_relu(0)
+        a_relu(1)
         for n in range(4):
             g_mult(0, 1, n)
             if n == 1:
-                a_half(4, 0)
+                a_mult(4, 0)
         g_quant(1, 0)
-        g_group(0, 1, 0, VE)
-        g_group(0, 1, 1, SC)
-        a_relu(1)
-        a_scale(4, 0)
-        g_group(0, 1, 2, VE)
-        g_group(0, 1, 3, SC)
+        g_group(0, 1, 0, VECTOR)
+        g_group(0, 1, 1, VECTOR)
+        a_weigh(4, 0)
+        g_group(0, 1, 2, SCALAR)
+        g_group(0, 1, 3, SCALAR)
         for n in range(4):
             g_mult(1, 1, n)
             if n == 1:
-                a_half(4, 1)
-        g_group(1, 1, 0, SC)
-        g_group(1, 1, 1, SC)
-        a_scale(4, 1)
-        g_group(1, 1, 2, SC)
-        g_group(1, 1, 3, SC)
+                a_mult(4, 1)
+        g_group(1, 1, 0, VECTOR)
         a_quant(0)
-        a_half(5, 0)
-        a_half(5, 1)
-        a_scale(5, 0)
-        a_scale(5, 1)
+        g_group(1, 1, 1, SCALAR)
+        a_weigh(4, 1)
+        g_group(1, 1, 2, SCALAR)
+        g_group(1, 1, 3, SCALAR)
+        a_mult(5, 0)
+        a_mult(5, 1)
         g_quant(0, 1)
+        a_weigh(5, 0)
+        a_weigh(5, 1)
         g_quant(1, 1)
-        turn["head"] = 0
-        for i in range(2, 6):
+        roles_fixed.append(True)
+        for i in range(2, 2 * LAG):
             a_turn(i)
         a_relu(2)
         a_relu(3)
 
-        def halves(q):
-            return [(i, h) for i in (2 * q, 2 * q + 1) for h in range(2)]
-
-        def update(q, engines):
-            for (i, h), engine in zip(halves(q), engines):
-                y_half(i, h)
-                y_step(i, h)
-                if engine == "gpsimd":
-                    y_round(i, h, engine)
+        def update_pair(q, rounded_by_gpsimd):
+            halves = [(i, h) for i in (2 * q, 2 * q + 1) for h in range(2)]
+            for n, (i, h) in enumerate(halves):
+                y_update(i, h)
+                if n < rounded_by_gpsimd:
+                    y_round(i, h, GPSIMD)
                 if h == 1:
                     y_store(i)
 
-        def y_planes(q):
-            y_quant(q, 0)
-            y_quant(q, 1)
-
         for s in range(LAG, PAIRS):
-            j = s - LAG
-            update(j, ["gpsimd"] * 4)
+            q = s - LAG
+            update_pair(q, 4)
             for i in (2 * s, 2 * s + 1):
                 for g in range(2):
-                    a_half(i, g)
-                    a_scale(i, g)
+                    a_mult(i, g)
+                    a_weigh(i, g)
             a_relu(2 * s - 2)
             a_relu(2 * s - 1)
-            if j > 0:
-                y_group(j - 1, 0, "scalar")
-                y_group(j - 1, 1, "scalar")
+            if q > 0:
+                y_group(q - 1, 0)
+                y_group(q - 1, 1)
             if s + 1 < PAIRS:
-                w_group(s + 1, 0, "scalar")
-                w_group(s + 1, 1, "scalar")
+                w_group(s + 1, 0, SCALAR)
+                w_group(s + 1, 1, SCALAR)
             if s == LAG:
                 a_quant(s - 2)
             a_quant(s - 1)
-            if j > 0:
-                y_planes(j - 1)
+            if q > 0:
+                y_planes(q - 1)
             if s + 1 < PAIRS:
                 w_quant(s + 1)
-            y_turn(j, 0)
+            y_turn(q, 0)
             a_turn(2 * s)
-            y_turn(j, 1)
+            y_turn(q, 1)
             a_turn(2 * s + 1)
 
         last = PAIRS - 1
         a_relu(2 * last)
         a_relu(2 * last + 1)
-        y_group(last - 3, 0, "scalar")
-        y_group(last - 3, 1, "scalar")
-        for q in (last - 2, last - 1):
-            update(q, ["gpsimd", "gpsimd", "scalar", "scalar"])
-            if q == last - 1:
-                for g in range(2):
-                    y_turn(q - 1, g)
-                    y_group(q - 1, g, "scalar")
-            for h in range(2):
-                y_round(2 * q + 1, h, "scalar")
-            if q == last - 2:
-                a_quant(last)
-                y_planes(last - 3)
-        update(last, ["gpsimd", "scalar", "scalar", "scalar"])
-        y_round(2 * last, 1, "scalar")
-        y_round(2 * last + 1, 0, "vector")
-        y_round(2 * last + 1, 1, "vector")
+        y_group(last - 3, 0)
+        y_group(last - 3, 1)
+        update_pair(last - 2, 2)
+        for h in range(2):
+            y_round(2 * (last - 2) + 1, h, SCALAR)
+        a_quant(last)
+        y_planes(last - 3)
+        update_pair(last - 1, 2)
+        for h in range(2):
+            y_turn(last - 2, h)
+            y_group(last - 2, h)
+        for h in range(2):
+            y_round(2 * (last - 1) + 1, h, SCALAR)
+        update_pair(last, 1)
+        y_round(2 * last, 1, SCALAR)
+        for h in range(2):
+            y_round(2 * last + 1, h, VECTOR)
         y_planes(last - 2)
         for q in (last - 1, last):
-            for g in range(2):
-                y_turn(q, g)
-                y_group(q, g, "scalar")
+            for h in range(2):
+                y_turn(q, h)
+                y_group(q, h)
         y_planes(last - 1)
         y_planes(last)

@@ -72,7 +72,7 @@ def tile_sae_decoder_logit_step_h3_kernel(
                 nc.vector.tensor_copy(out=out, in_=in_)
 
         tw_raw = keep.tile([P, 2, 4], BF16, name="tw_raw")
-        nc.sync.dma_start(out=tw_raw[:], in_=token_weight.rearrange("(g p t) -> p g t", g=2, t=4))
+        nc.scalar.dma_start(out=tw_raw[:], in_=token_weight.rearrange("(g p t) -> p g t", g=2, t=4))
         rows_raw = keep.tile([2 * TILES, P], BF16, name="rows_raw")
         nc.scalar.dma_start(out=rows_raw[0:TILES, :], in_=b_enc.rearrange("(i p) -> i p", p=P))
         nc.scalar.dma_start(out=rows_raw[TILES : 2 * TILES, :], in_=step.rearrange("(i p) -> i p", p=P))

from contextlib import ExitStack

import concourse.mybir as mybir
from concourse.masks import make_identity

T, D, F, V = 1024, 1024, 2048, 512
FLOPS = 2 * T * D * F + 2 * T * V * D + 2 * F * T * D

F32 = mybir.dt.float32
BF16 = mybir.dt.bfloat16
U32 = mybir.dt.uint32
I32 = mybir.dt.int32
U8 = mybir.dt.uint8
FP8X4 = mybir.dt.float8_e4m3fn_x4
ALU = mybir.AluOpType
ACT = mybir.ActivationFunctionType
VECTOR, SCALAR, GPSIMD = "vector", "scalar", "gpsimd"

P = 128
KP = 512
HALF = 256
TILES = F // P
PAIRS = TILES // 2
LAG = 3
CODE_STORES = ((0, 4), (4, 8), (8, 10), (10, 12), (12, 14), (14, 16))
SCALE_STORES = ((0, 8), (8, 16))
BANKS = {"product": (0, 1, 2, 3), "turn": (4, 5, 6, 7), "any": (0, 1, 2, 3, 4, 5, 6, 7)}


def tile_sae_decoder_logit_step_h3_kernel(
    tc, x, w_enc, b_enc, token_weight, logit_cotangent, w_unembed, w_dec, step, out_0, out_1, out_2
):
    nc = tc.nc
    with ExitStack() as ctx:
        keep = ctx.enter_context(tc.tile_pool(name="keep", bufs=1))
        work = ctx.enter_context(tc.tile_pool(name="work", bufs=3))
        psum = ctx.enter_context(tc.psum_pool(name="psum", bufs=1))
        ctx.enter_context(tc.manual_schedule())

        banks_taken = {"product": 0, "turn": 0, "any": 0}
        roles_fixed = []
        tiles = {}

        def bank(role):
            role = role if roles_fixed else "any"
            number = BANKS[role][banks_taken[role] % len(BANKS[role])]
            banks_taken[role] = banks_taken[role] + 1
            return psum.tile([P, KP], F32, name="bank%d" % number)

        def mx_operand(name, pool=keep, bufs=None):
            codes = pool.tile([P, KP], U32, name=name + "_codes", align_bytes=64, bufs=bufs)
            scales = pool.tile([P, KP], U8, name=name + "_scales", align_bytes=64, bufs=bufs)
            return codes, scales

        def multiply(out, stationary, s_first, moving, m_first, width, start, stop):
            s_cols = slice(s_first, s_first + P)
            m_cols = slice(m_first, m_first + width)
            nc.tensor.matmul_mx(
                out=out,
                lhsT=stationary[0][:, s_cols].bitcast(FP8X4),
                lhsT_scale=stationary[1][:, s_cols],
                rhs=moving[0][:, m_cols].bitcast(FP8X4),
                rhs_scale=moving[1][:, m_cols],
                start=start,
                stop=stop,
            )

        def copy_on(engine, out, in_):
            if engine == SCALAR:
                nc.scalar.copy(out=out, in_=in_)
            else:
                nc.vector.tensor_copy(out=out, in_=in_)

        tw_raw = keep.tile([P, 2, 4], BF16, name="tw_raw")
        nc.scalar.dma_start(out=tw_raw[:], in_=token_weight.rearrange("(g p t) -> p g t", g=2, t=4))
        rows_raw = keep.tile([2 * TILES, P], BF16, name="rows_raw")
        nc.scalar.dma_start(out=rows_raw[0:TILES, :], in_=b_enc.rearrange("(i p) -> i p", p=P))
        nc.scalar.dma_start(out=rows_raw[TILES : 2 * TILES, :], in_=step.rearrange("(i p) -> i p", p=P))

        x_raw, w_raw, lc_raw, wu_raw, wd_raw = {}, {}, {}, {}, {}

        def load_x(g, u):
            x_raw[g, u] = keep.tile([P, 2, D], BF16, name="x_raw%d%d" % (g, u))
            rows = x[KP * g : KP * (g + 1), :].rearrange("(p u e) d -> p u e d", u=2, e=2)
            nc.sync.dma_start(out=x_raw[g, u][:], in_=rows[:, u, :, :])

        def load_w(chunk):
            for c in range(2):
                w_raw[chunk, c] = keep.tile([P, 4, KP], BF16, name="w_raw%d%d" % (chunk, c))
                rows = w_enc[KP * c : KP * (c + 1), KP * chunk : KP * (chunk + 1)]
                nc.sync.dma_start(out=w_raw[chunk, c][:], in_=rows.rearrange("(p t) f -> p t f", t=4))

        def load_lc(g):
            lc_raw[g] = keep.tile([P, 4, V], BF16, name="lc_raw%d" % g)
            rows = logit_cotangent[KP * g : KP * (g + 1), :]
            nc.sync.dma_start(out=lc_raw[g][:], in_=rows.rearrange("(p t) v -> p t v", t=4))

        def load_wu(h):
            wu_raw[h] = keep.tile([P, 2, 2, V], BF16, name="wu_raw%d" % h)
            rows = w_unembed[KP * h : KP * (h + 1), :]
            nc.sync.dma_start(out=wu_raw[h][:], in_=rows.rearrange("(a p e) v -> p a e v", a=2, e=2))

        def load_wd(q):
            wd_raw[q] = work.tile([P, 2, D], BF16, name="wd_raw", bufs=LAG)
            rows = w_dec[HALF * q : HALF * (q + 1), :]
            nc.sync.dma_start(out=wd_raw[q][:], in_=rows.rearrange("(a p) d -> p a d", a=2))

        load_lc(0)
        load_wu(0)
        load_x(0, 0)
        load_x(0, 1)
        load_w(0)
        load_x(1, 0)
        load_x(1, 1)
        load_lc(1)
        load_wu(1)
        for chunk in range(1, 4):
            load_w(chunk)
            load_wd(chunk - 1)

        ident = keep.tile([P, P], F32, name="ident")
        make_identity(nc, ident[:])
        rows32 = keep.tile([P, P], F32, name="rows32")
        nc.gpsimd.memset(rows32[:], 0.0)
        tw32 = keep.tile([P, 8], F32, name="tw32")
        half_sign = keep.tile([P, 8], F32, name="half_sign")
        bias = keep.tile([P, TILES], F32, name="bias")
        minus_step = keep.tile([P, TILES], F32, name="minus_step")
        tw_abs = keep.tile([P, T], BF16, name="tw_abs")

        def widen_vectors():
            weights = tw_raw[:].rearrange("p g t -> p (g t)")
            nc.vector.tensor_scalar(
                out=half_sign[:], in0=weights, scalar1=0.0, scalar2=0.5, op0=ALU.is_ge, op1=ALU.subtract
            )
            nc.vector.tensor_copy(out=tw32[:], in_=weights)
            nc.vector.tensor_copy(out=rows32[0 : 2 * TILES, :], in_=rows_raw[:])

        def spread_weights(g):
            spread = bank("product")
            for t in range(4):
                column = tw32[:, 4 * g + t : 4 * g + t + 1].to_broadcast([P, P])
                nc.tensor.transpose(spread[:, P * t : P * (t + 1)], column, ident[:])
            nc.scalar.activation(
                out=tw_abs[:, KP * g : KP * (g + 1)].rearrange("m (u p e) -> m u p e", u=2, e=2),
                in_=spread[:].rearrange("m (u e p) -> m u p e", u=2, e=2),
                func=ACT.Abs,
            )

        def turn_vectors():
            turned = bank("product")
            nc.tensor.transpose(turned[:, 0:P], rows32[:], ident[:])
            nc.vector.tensor_copy(out=bias[:], in_=turned[:, 0:TILES])
            nc.vector.tensor_scalar(
                out=minus_step[:], in0=turned[:, TILES : 2 * TILES], scalar1=-1.0, scalar2=None, op0=ALU.mult
            )

        def grouped_half(key, half):
            if key not in tiles:
                tiles[key] = work.tile([P, 4 * KP], BF16, name="grouped", bufs=5, align_bytes=64)
            return tiles[key][:, 4 * HALF * half : 4 * HALF * (half + 1)]

        def quantize(key, operand, halves=(0, 1)):
            codes, scales = operand
            first, end = HALF * halves[0], HALF * (halves[-1] + 1)
            nc.vector.quantize_mx(
                out=codes[:, first:end].bitcast(FP8X4),
                scales=scales[:, first:end],
                in_=tiles[key][:, 4 * first : 4 * end],
            )

        def turn_four(sources):
            turned = bank("turn")
            for n in range(4):
                nc.tensor.transpose(turned[:, P * n : P * (n + 1)], sources[n], ident[:])
            return turned

        def sort_pairs(key, words):
            ordered = work.tile([P, KP], F32, name="ordered", bufs=4)
            tiles["sorted", key] = ordered
            nc.vector.tensor_copy(
                out=ordered[:].rearrange("k (e w p) -> k e w p", e=2, w=2),
                in_=words.rearrange("k e (p w) -> k e w p", w=2),
            )

        def turn_two_rows(key, words):
            if ("sorted", key) in tiles:
                sources = [tiles["sorted", key][:, P * n : P * (n + 1)] for n in range(4)]
            else:
                sources = [words[:, e, w:HALF:2] for e in range(2) for w in range(2)]
            tiles["turned", key] = turn_four(sources)

        def group_two_rows(key, target):
            nc.scalar.copy(
                out=target.bitcast(F32).rearrange("k (p e w) -> k p e w", e=2, w=2),
                in_=tiles["turned", key][:].rearrange("k (e w p) -> k p e w", e=2, w=2),
            )

        x_q = {(g, c): mx_operand("x%d%d" % (g, c)) for g in range(2) for c in range(2)}
        lc_q = {g: mx_operand("lc%d" % g) for g in range(2)}
        wu_q = {h: mx_operand("wu%d" % h) for h in range(2)}
        g_q = {(g, h): mx_operand("g%d%d" % (g, h)) for g in range(2) for h in range(2)}
        w_q, a_q = {}, {}

        def x_words(g, u, c):
            return x_raw[g, u][:].bitcast(F32)[:, :, HALF * c : HALF * (c + 1)]

        def x_sort(g, u, c):
            sort_pairs(("x", g, u, c), x_words(g, u, c))

        def x_turn(g, u, c):
            turn_two_rows(("x", g, u, c), x_words(g, u, c))

        def x_group(g, u, c):
            group_two_rows(("x", g, u, c), grouped_half(("x", g, c), u))

        def x_quant(g, c):
            quantize(("x", g, c), x_q[g, c])

        def lc_sign(g):
            signed = work.tile([P, 4, V], BF16, name="signed", bufs=1)
            tiles["signed", g] = signed
            for t in range(4):
                nc.vector.tensor_scalar(
                    out=signed[:, t, :].rearrange("p (w c e) -> p w c e", w=2, e=2),
                    in0=lc_raw[g][:, t, :].rearrange("p (c w e) -> p w c e", w=2, e=2),
                    scalar1=half_sign[:, 4 * g + t : 4 * g + t + 1],
                    scalar2=2.0,
                    op0=ALU.mult,
                    op1=ALU.mult,
                )

        def lc_turn(g, a):
            words = tiles["signed", g][:].rearrange("p t v -> p (t v)").bitcast(F32)
            turned = turn_four([words[:, P * n : P * (n + 1)] for n in range(4 * a, 4 * a + 4)])
            nc.scalar.copy(
                out=grouped_half(("lc", g), a).bitcast(F32).rearrange("k (j p w) -> k j p w", j=2, w=2),
                in_=turned[:].rearrange("k (j w p) -> k j p w", j=2, w=2),
            )

        def wu_words(h, a):
            return wu_raw[h][:].bitcast(F32)[:, a, :, :]

        def wu_turn(h, a):
            turn_two_rows(("wu", h, a), wu_words(h, a))
            group_two_rows(("wu", h, a), grouped_half(("wu", h), a))

        def g_mult(g, h, n):
            acc = bank("product")
            tiles["g", g, h, n] = acc
            for t in range(4):
                multiply(acc[:, P * t : P * (t + 1)], lc_q[g], P * t, wu_q[h], P * n, P, True, True)

        def g_group(g, h, n, engine):
            target = grouped_half(("g", g, h), n // 2)[:, KP * (n % 2) : KP * (n % 2 + 1)]
            copy_on(
                engine,
                target.rearrange("p (d t) -> p d t", t=4),
                tiles["g", g, h, n][:].rearrange("p (t d) -> p d t", t=4),
            )

        def g_quant(g, h):
            quantize(("g", g, h), g_q[g, h])

        def w_group(q, c, engine):
            if c == 0:
                tiles["w", q] = work.tile([P, 4 * KP], BF16, name="w_grouped", bufs=2, align_bytes=64)
            cols = slice(HALF * (q % 2), HALF * (q % 2 + 1))
            copy_on(
                engine,
                tiles["w", q][:, 4 * HALF * c : 4 * HALF * (c + 1)].rearrange("p (a i t) -> p a t i", i=4, t=4),
                w_raw[q // 2, c][:, :, cols].rearrange("p t (a i) -> p a t i", i=4),
            )

        def w_quant(q):
            w_q[q] = mx_operand("w", work, 3)
            quantize(("w", q), w_q[q])

        def a_mult(i, g):
            acc = bank("product")
            tiles["pre", i, g] = acc
            for c in range(2):
                multiply(acc[:], w_q[i // 2], HALF * c + P * (i % 2), x_q[g, c], 0, KP, c == 0, c == 1)

        def a_weigh(i, g):
            if g == 0:
                tiles["weighed", i] = work.tile([P, T], BF16, name="a_t", bufs=5)
            cols = slice(KP * g, KP * (g + 1))
            nc.vector.scalar_tensor_tensor(
                out=tiles["weighed", i][:, cols],
                in0=tiles["pre", i, g][:],
                scalar=bias[:, i : i + 1],
                in1=tw_abs[:, cols],
                op0=ALU.add,
                op1=ALU.mult,
            )

        def a_turn(i):
            words = tiles["weighed", i][:].bitcast(F32)
            starts = [HALF * g + P * u for u in range(2) for g in range(2)]
            tiles["a_turned", i] = turn_four([words[:, first : first + P] for first in starts])

        def a_relu(i):
            nc.scalar.activation(
                out=grouped_half(("a", i // 2), i % 2).rearrange("p (m u e) -> p m u e", u=2, e=2),
                in_=tiles["a_turned", i][:].bitcast(BF16).rearrange("p (u m e) -> p m u e", u=2, e=2),
                func=ACT.Relu,
            )

        def a_quant(q):
            a_q[q] = mx_operand("a", work, LAG + 1)
            quantize(("a", q), a_q[q])

        def y_update(i, h):
            acc = bank("product")
            for g in range(2):
                multiply(acc[:], a_q[i // 2], HALF * (i % 2) + P * g, g_q[g, h], 0, KP, g == 0, g == 1)
            if h == 0:
                tiles["y", i] = work.tile([P, D], F32, name="y", bufs=7)
            cols = slice(KP * h, KP * (h + 1))
            nc.vector.scalar_tensor_tensor(
                out=tiles["y", i][:, cols],
                in0=acc[:],
                scalar=minus_step[:, i : i + 1],
                in1=wd_raw[i // 2][:, i % 2, cols],
                op0=ALU.mult,
                op1=ALU.add,
            )

        def y_store(i):
            nc.sync.dma_start(out=out_0[P * i : P * (i + 1), :], in_=tiles["y", i][:])
            if i % 2 == 1 and i // 2 + LAG < PAIRS:
                load_wd(i // 2 + LAG)

        def y_round(i, h, engine):
            rounded = work.tile([P, KP], BF16, name="y_rounded", bufs=8)
            tiles["rounded", i, h] = rounded
            out = rounded[:].rearrange("m (u c e) -> m u c e", u=2, e=2)
            in_ = tiles["y", i][:, KP * h : KP * (h + 1)].rearrange("m (c u e) -> m u c e", u=2, e=2)
            if engine == GPSIMD:
                nc.gpsimd.tensor_scalar(out=out, in0=in_, scalar1=1.0, scalar2=1.0, op0=ALU.mult, op1=ALU.mult)
            else:
                copy_on(engine, out, in_)

        def y_turn(q, h):
            words = [tiles["rounded", 2 * q + a, h][:].bitcast(F32) for a in range(2)]
            tiles["y_turned", q, h] = turn_four([words[a][:, P * u : P * (u + 1)] for a in range(2) for u in range(2)])

        def y_group(q, h):
            grouped = work.tile([P, 4 * HALF], BF16, name="y_grouped", bufs=4, align_bytes=64)
            tiles["y_grouped", q, h] = grouped
            nc.scalar.copy(
                out=grouped[:].bitcast(F32).rearrange("p (a m u) -> p a m u", a=2, u=2),
                in_=tiles["y_turned", q, h][:].rearrange("p (a u m) -> p a m u", a=2, u=2),
            )

        codes_out = out_1.rearrange("g p m t -> p g (m t)").bitcast(I32)
        scales_out = out_2.rearrange("g r m -> r g m").bitcast(I32)
        code_store = {i: (first, end) for first, end in CODE_STORES for i in range(first, end)}
        scale_store = {i: (first, end) for first, end in SCALE_STORES for i in range(first, end)}

        def y_planes(q):
            first, end = 2 * q, 2 * q + 2
            c_first, c_end = code_store[first]
            s_first, s_end = scale_store[first]
            if first == c_first:
                width = P * (c_end - c_first)
                tiles["y_codes"] = work.tile([P, 2, width], U32, name="y_codes", bufs=3, align_bytes=64)
            if first == s_first:
                width = P * (s_end - s_first)
                tiles["y_scales"] = keep.tile([P, 2, width], U8, name="y_scales%d" % s_first, align_bytes=64)
            codes, scales = tiles["y_codes"], tiles["y_scales"]
            for h in range(2):
                nc.vector.quantize_mx(
                    out=codes[:, h, P * (first - c_first) : P * (end - c_first)].bitcast(FP8X4),
                    scales=scales[:, h, P * (first - s_first) : P * (end - s_first)],
                    in_=tiles["y_grouped", q, h][:],
                )
            if end == c_end:
                nc.sync.dma_start(out=codes_out[:, :, P * c_first : P * c_end], in_=codes[:].bitcast(I32))
            if end == s_end:
                queue = nc.scalar if end == TILES else nc.sync
                for quad in range(4):
                    queue.dma_start(
                        out=scales_out[4 * quad : 4 * quad + 4, :, P * s_first // 4 : P * s_end // 4],
                        in_=scales[32 * quad : 32 * quad + 4, :, :].bitcast(I32),
                    )

        widen_vectors()
        spread_weights(0)
        spread_weights(1)
        lc_sign(0)
        lc_turn(0, 0)
        lc_turn(0, 1)
        for a in range(2):
            sort_pairs(("wu", 0, a), wu_words(0, a))
        for c in range(2):
            x_sort(0, 0, c)
        quantize(("lc", 0), lc_q[0])
        wu_turn(0, 0)
        wu_turn(0, 1)
        quantize(("wu", 0), wu_q[0], (0,))
        for c in range(2):
            x_turn(0, 0, c)
            x_group(0, 0, c)
        quantize(("wu", 0), wu_q[0], (1,))
        turn_vectors()
        w_group(1, 0, SCALAR)
        w_group(0, 0, VECTOR)
        w_group(0, 1, VECTOR)
        w_group(1, 1, VECTOR)
        for n in range(2):
            g_mult(0, 0, n)
            g_group(0, 0, n, SCALAR)
        for g, u in ((0, 1), (1, 0)):
            for c in range(2):
                x_turn(g, u, c)
                x_group(g, u, c)
        w_quant(0)
        x_quant(0, 0)
        x_quant(0, 1)
        w_quant(1)
        for n in range(2, 4):
            g_mult(0, 0, n)
            g_group(0, 0, n, SCALAR)
        lc_sign(1)
        for i in range(2):
            a_mult(i, 0)
            a_weigh(i, 0)
        g_quant(0, 0)
        w_group(2, 0, SCALAR)
        w_group(3, 0, VECTOR)
        w_group(2, 1, VECTOR)
        for c in range(2):
            x_turn(1, 1, c)
            x_group(1, 1, c)
            x_quant(1, c)
        lc_turn(1, 0)
        lc_turn(1, 1)
        w_group(3, 1, SCALAR)
        a_mult(2, 0)
        a_mult(3, 0)
        a_weigh(2, 0)
        quantize(("lc", 1), lc_q[1])
        a_weigh(3, 0)
        wu_turn(1, 0)
        wu_turn(1, 1)
        for i in range(4):
            a_mult(i, 1)
            g_mult(1, 0, i)
            a_weigh(i, 1)
            g_group(1, 0, i, SCALAR)
            if i == 0:
                w_quant(2)
                quantize(("wu", 1), wu_q[1])
        w_quant(3)
        a_turn(0)
        a_turn(1)
        a_relu(0)
        a_relu(1)
        for n in range(4):
            g_mult(0, 1, n)
            if n == 1:
                a_mult(4, 0)
        g_quant(1, 0)
        g_group(0, 1, 0, VECTOR)
        g_group(0, 1, 1, VECTOR)
        a_weigh(4, 0)
        g_group(0, 1, 2, SCALAR)
        g_group(0, 1, 3, SCALAR)
        for n in range(4):
            g_mult(1, 1, n)
            if n == 1:
                a_mult(4, 1)
        g_group(1, 1, 0, VECTOR)
        a_quant(0)
        g_group(1, 1, 1, SCALAR)
        a_weigh(4, 1)
        g_group(1, 1, 2, SCALAR)
        g_group(1, 1, 3, SCALAR)
        a_mult(5, 0)
        a_mult(5, 1)
        g_quant(0, 1)
        a_weigh(5, 0)
        a_weigh(5, 1)
        g_quant(1, 1)
        roles_fixed.append(True)
        for i in range(2, 2 * LAG):
            a_turn(i)
        a_relu(2)
        a_relu(3)

        def update_pair(q, rounded_by_gpsimd):
            halves = [(i, h) for i in (2 * q, 2 * q + 1) for h in range(2)]
            for n, (i, h) in enumerate(halves):
                y_update(i, h)
                if n < rounded_by_gpsimd:
                    y_round(i, h, GPSIMD)
                if h == 1:
                    y_store(i)

        for s in range(LAG, PAIRS):
            q = s - LAG
            update_pair(q, 4)
            for i in (2 * s, 2 * s + 1):
                for g in range(2):
                    a_mult(i, g)
                    a_weigh(i, g)
            a_relu(2 * s - 2)
            a_relu(2 * s - 1)
            if q > 0:
                y_group(q - 1, 0)
                y_group(q - 1, 1)
            if s + 1 < PAIRS:
                w_group(s + 1, 0, SCALAR)
                w_group(s + 1, 1, SCALAR)
            if s == LAG:
                a_quant(s - 2)
            a_quant(s - 1)
            if q > 0:
                y_planes(q - 1)
            if s + 1 < PAIRS:
                w_quant(s + 1)
            y_turn(q, 0)
            a_turn(2 * s)
            y_turn(q, 1)
            a_turn(2 * s + 1)

        last = PAIRS - 1
        a_relu(2 * last)
        a_relu(2 * last + 1)
        y_group(last - 3, 0)
        y_group(last - 3, 1)
        update_pair(last - 2, 2)
        for h in range(2):
            y_round(2 * (last - 2) + 1, h, SCALAR)
        a_quant(last)
        y_planes(last - 3)
        update_pair(last - 1, 2)
        for h in range(2):
            y_turn(last - 2, h)
            y_group(last - 2, h)
        for h in range(2):
            y_round(2 * (last - 1) + 1, h, SCALAR)
        update_pair(last, 1)
        y_round(2 * last, 1, SCALAR)
        for h in range(2):
            y_round(2 * last + 1, h, VECTOR)
        y_planes(last - 2)
        for q in (last - 1, last):
            for h in range(2):
                y_turn(q, h)
                y_group(q, h)
        y_planes(last - 1)
        y_planes(last)
